import numpy as np
import ml_dtypes


def mxq(x, axis, fmt="e4m3"):
    dtype, down = {"e4m3": (ml_dtypes.float8_e4m3fn, 7), "e5m2": (ml_dtypes.float8_e5m2, 14)}[fmt]
    v = np.moveaxis(np.asarray(x, np.float32).astype(ml_dtypes.bfloat16).astype(np.float64), axis, -1)
    blocks = v.reshape(v.shape[:-1] + (-1, 32))
    amax = np.abs(blocks).max(-1, keepdims=True)
    byte = np.maximum(np.where(amax > 0, np.frexp(amax)[1] - 1 + 127, 0) - down, 1)
    scale = np.exp2(byte - 127.0)
    codes = (blocks / scale).astype(np.float32).astype(dtype).astype(np.float64)
    return np.moveaxis((codes * scale).reshape(v.shape), -1, axis)


WIDE = False


def mx_kscale(k):
    if not WIDE:
        return np.ones(k)
    levels = np.array([10, -10, 5, -5, 0])
    if k % 512:
        return np.exp2(np.random.permutation(np.resize(levels, k // 32))).repeat(32)
    a = np.empty((k // 512, 16))
    for p in range(k // 512):
        a[p, :8] = np.random.permutation(np.resize(levels, 8))
        for g in range(8):
            far = levels[np.abs(levels - a[p, g]) >= 10]
            a[p, g + 8] = far[np.random.randint(len(far))]
    return np.exp2(a.ravel()).repeat(32)


def f64(x):
    return np.asarray(x).astype(np.float64)


def striped(idx):
    return np.tile(idx.reshape(-1, 16).T, (8, 1)).astype(np.uint16)


def unstriped(offs):
    return offs[:16].T.reshape(-1).astype(np.int64)


E2M1 = np.array([0.0, 0.5, 1.0, 1.5, 2.0, 3.0, 4.0, 6.0, -0.0, -0.5, -1.0, -1.5, -2.0, -3.0, -4.0, -6.0])


def pack_weight(w, fmt):
    k, n = w.shape
    w = f64(np.asarray(w, np.float32).astype(ml_dtypes.bfloat16)).reshape(k // 32, 32, n)
    amax = np.abs(w).max(1)
    if fmt == "e4m3":
        byte = np.frexp(amax)[1] - 1 + 127 - 7
    else:
        mant, ex = np.frexp(amax / 6.0)
        byte = np.where(mant > 0.5, ex, ex - 1) + 127
    byte = np.clip(np.where(amax > 0, byte, 1), 1, 254)
    scaled = (w * np.exp2(127.0 - byte)[:, None, :]).reshape(k, n).astype(np.float32)
    by_word = np.ascontiguousarray(scaled.reshape(k // 512, 128, 4, n).transpose(0, 1, 3, 2))
    if fmt == "e4m3":
        words = by_word.astype(ml_dtypes.float8_e4m3fn).view(np.uint8)
    else:
        c = by_word.astype(ml_dtypes.float4_e2m1fn).view(np.uint8) & 0xF
        words = (c[..., 0::2] | (c[..., 1::2] << 4)).reshape(k // 512, 128, 2 * n)
    return np.ascontiguousarray(words), np.ascontiguousarray(byte.astype(np.uint8).reshape(k // 512, 16, n))


def unpack_weight(words, scales, fmt):
    g, _, n = scales.shape
    words = np.ascontiguousarray(words).reshape(g, 128, n, -1)
    if fmt == "e4m3":
        vals = words.view(ml_dtypes.float8_e4m3fn).astype(np.float64)
    else:
        nib = np.empty((g, 128, n, 4), np.uint8)
        nib[..., 0::2] = words & 0xF
        nib[..., 1::2] = words >> 4
        vals = E2M1[nib]
    vals = vals * np.repeat(np.exp2(scales.astype(np.float64) - 127.0), 8, axis=1)[..., None]
    return vals.transpose(0, 1, 3, 2).reshape(g * 512, n)


def gelu(v):
    return 0.5 * v * (1.0 + np.tanh(np.sqrt(2.0 / np.pi) * (v + 0.044715 * v**3)))


K, H, N, T, S, P, P2 = 1536, 1024, 512, 2048, 1024, 512, 256

def setup_inputs():
    n = np.random.standard_normal
    s = mx_kscale(K)[:, None]
    u = mx_kscale(H)[:, None]
    tab_words, tab_scales = pack_weight(n((K, T)) * s, "e4m3")
    w1 = (0.3 * n((K, H)) / np.sqrt(K) / s).astype(np.float32)
    sign = np.where(np.random.uniform(size=H) < 0.5, -1.0, 1.0)
    phase = (sign * np.random.uniform(0.8, 1.2, H)).astype(np.float32)
    gain = (4.0 * np.exp(0.3 * n(H)) * u[:, 0]).astype(np.float32)
    w2_words, w2_scales = pack_weight(n((H, N)) / np.sqrt(H) / u, "e2m1")
    links = np.random.permutation(S)
    sides = np.random.permutation(P)
    return {"tab_words": tab_words, "tab_scales": tab_scales,
            "offs": striped(np.random.permutation(T)[:S]),
            "w1": w1, "phase": phase, "gain": gain,
            "pos1": striped(links[:P]), "pos2": striped(links[P:]),
            "w2_words": w2_words, "w2_scales": w2_scales,
            "pos3": striped(sides[:P2]), "pos4": striped(sides[P2:])}

def reference(tab_words, tab_scales, offs, w1, phase, gain, pos1, pos2,
              w2_words, w2_scales, pos3, pos4):
    v = unpack_weight(tab_words, tab_scales, "e4m3")[:, unstriped(offs)]
    a = mxq(f64(w1), 0, "e4m3").T @ v
    h = np.cos(a + f64(phase)[:, None])
    z = h[:, unstriped(pos1)] * h[:, unstriped(pos2)] * f64(gain)[:, None]
    w2 = unpack_weight(w2_words, w2_scales, "e2m1")
    y = w2.T @ mxq(z, 0, "e4m3")
    d = y[:, unstriped(pos3)] - y[:, unstriped(pos4)]
    return d * d

@@ -1,0 +1,218 @@
+import math
+from contextlib import ExitStack
+
+import concourse.mybir as mybir
+
+K, H, N, T, S, PAIRS, CONTRASTS = 1536, 1024, 512, 2048, 1024, 512, 256
+FLOPS = 2 * K * H * S + 2 * H * N * PAIRS
+
+F32 = mybir.dt.float32
+BF16 = mybir.dt.bfloat16
+I32 = mybir.dt.int32
+U32 = mybir.dt.uint32
+U16 = mybir.dt.uint16
+U8 = mybir.dt.uint8
+FP8X4 = mybir.dt.float8_e4m3fn_x4
+FP4X4 = mybir.dt.float4_e2m1fn_x4
+ACT = mybir.ActivationFunctionType
+ALU = mybir.AluOpType
+
+P = 128
+PACK = 4
+PASS = P * PACK
+BANK = 512
+K_PASSES = K // PASS
+H_PASSES = H // PASS
+
+
+def tile_list_echo_chamber_contrast_kernel(
+    tc, tab_words, tab_scales, offs, w1, phase, gain, pos1, pos2, w2_words, w2_scales, pos3, pos4, out
+):
+    nc = tc.nc
+    with ExitStack() as ctx:
+        held = ctx.enter_context(tc.tile_pool(name="held", bufs=1))
+        ring = ctx.enter_context(tc.tile_pool(name="ring", bufs=3))
+        psum = ctx.enter_context(tc.psum_pool(name="psum", bufs=8))
+
+        def load_list(name, src):
+            t = held.tile(list(src.shape), U16, name=name)
+            nc.sync.dma_start(t[:], src)
+            return t
+
+        def load_table_words(a):
+            t = held.tile([P, T], I32, name="tab_words_%d" % a)
+            nc.sync.dma_start(t[:], tab_words[a].rearrange("p t i -> p (t i)").bitcast(I32))
+            return t
+
+        def load_w1(a, c0, c1):
+            t = held.tile([P, PACK, c1 - c0], F32, name="w1_raw_%d_%d" % (a, c0))
+            rows = w1[a * PASS : (a + 1) * PASS, c0:c1]
+            nc.sync.dma_start(t[:], rows.rearrange("(p j) c -> p j c", j=PACK))
+            return t
+
+        tab_planes = held.tile([P, T], U8, name="tab_planes")
+        nc.gpsimd.memset(tab_planes[:].bitcast(I32), 0)
+        for q in range(4):
+            nc.gpsimd.dma_start(
+                tab_planes[32 * q : 32 * q + 4 * K_PASSES, :].bitcast(I32),
+                tab_scales[:, 4 * q : 4 * q + 4, :].bitcast(I32),
+            )
+        gain_cols = held.tile([P, H_PASSES, PACK], F32, name="gain_cols")
+        phase_cols = held.tile([P, H_PASSES, PACK], F32, name="phase_cols")
+        nc.scalar.dma_start(gain_cols[:], gain.rearrange("(b p t) -> p b t", b=H_PASSES, t=PACK))
+        nc.scalar.dma_start(phase_cols[:], phase.rearrange("(b p t) -> p b t", b=H_PASSES, t=PACK))
+
+        words0 = load_table_words(0)
+        offs_sb = load_list("offs_sb", offs)
+        raw00 = load_w1(0, 0, PASS)
+        words1 = load_table_words(1)
+        raw10 = load_w1(1, 0, PASS)
+        words2 = load_table_words(2)
+        raw20a = load_w1(2, 0, PASS // 2)
+        raw20b = load_w1(2, PASS // 2, PASS)
+        pos1_sb = load_list("pos1_sb", pos1)
+        pos2_sb = load_list("pos2_sb", pos2)
+        raw_late = [load_w1(a, PASS, 2 * PASS) for a in range(K_PASSES)]
+        w2_codes = held.tile([P, H_PASSES, 2 * N], U8, name="w2_codes", align_bytes=64)
+        nc.sync.dma_start(w2_codes[:].bitcast(I32), w2_words.rearrange("b p c -> p b c").bitcast(I32))
+        pos3_sb = load_list("pos3_sb", pos3)
+        pos4_sb = load_list("pos4_sb", pos4)
+
+        w2_planes = held.tile([P, H_PASSES, N], U8, name="w2_planes", align_bytes=64)
+        nc.vector.memset(w2_planes[:].bitcast(I32), 0)
+        for q in range(4):
+            nc.sync.dma_start(
+                w2_planes[32 * q : 32 * q + 4, :, :].bitcast(I32),
+                w2_scales[:, 4 * q : 4 * q + 4, :].rearrange("b r c -> r b c").bitcast(I32),
+            )
+
+        gain_rows = []
+        for b in range(H_PASSES):
+            g = held.tile([P, PACK, PAIRS], F32, name="gain_rows_%d" % b)
+            gain_rows.append(g)
+
+        def spread_gain(b):
+            nc.scalar.copy(gain_rows[b][:], gain_cols[:, b, :].unsqueeze(2).to_broadcast([P, PACK, PAIRS]))
+
+        def gather_words(window, a):
+            t = held.tile([P, S], U32, name="v_codes_%d" % a, align_bytes=64)
+            nc.vector.tensor_copy(t[:], window[:].bitcast(U32).indirect(offs_sb[:]))
+            return t
+
+        def new_rounded():
+            return ring.tile([P, PACK * PASS], BF16, name="w1_rounded", align_bytes=64)
+
+        def round_w1(copy, rounded, raw, m0):
+            m1 = m0 + raw.shape[2] // PACK
+            dst = rounded[:].rearrange("p (t m j) -> p m j t", t=PACK, j=PACK)
+            copy(dst[:, m0:m1, :, :], raw[:].rearrange("p j (m t) -> p m j t", t=PACK))
+
+        def quantise_w1(rounded, name, cuts):
+            codes = held.tile([P, PASS], U32, name=name + "_codes", align_bytes=64)
+            plane = held.tile([P, PASS], U8, name=name + "_plane", align_bytes=64)
+            for c0, c1 in zip(cuts[:-1], cuts[1:]):
+                nc.vector.quantize_mx(
+                    codes[:, c0:c1].bitcast(FP8X4), plane[:, c0:c1], rounded[:, PACK * c0 : PACK * c1]
+                )
+            return codes, plane
+
+        v_codes = [None] * K_PASSES
+        w1_mx = {}
+        spread_gain(0)
+        v_codes[0] = gather_words(words0, 0)
+        v_planes = held.tile([P, S], U8, name="v_planes", align_bytes=64)
+        nc.vector.tensor_copy(v_planes[:], tab_planes[:].indirect(offs_sb[:]))
+        rounded = new_rounded()
+        round_w1(nc.scalar.copy, rounded, raw00, 0)
+        spread_gain(1)
+        v_codes[1] = gather_words(words1, 1)
+        w1_mx[0, 0] = quantise_w1(rounded, "w1_00", [0, PASS])
+        rounded = new_rounded()
+        round_w1(nc.scalar.copy, rounded, raw10, 0)
+        v_codes[2] = gather_words(words2, 2)
+        w1_mx[1, 0] = quantise_w1(rounded, "w1_10", [0, PASS])
+        rounded = new_rounded()
+        round_w1(nc.scalar.copy, rounded, raw20a, 0)
+        round_w1(nc.vector.tensor_copy, rounded, raw20b, P // 2)
+        w1_mx[2, 0] = quantise_w1(rounded, "w1_20", [0, P, 2 * P, PASS])
+
+        def first_pass(banks, a, b, t):
+            codes, plane = w1_mx[a, b]
+            for half in range(2):
+                cols = slice(half * BANK, (half + 1) * BANK)
+                nc.tensor.matmul_mx(
+                    banks[half][:],
+                    lhsT=codes[:, t * P : (t + 1) * P].bitcast(FP8X4),
+                    lhsT_scale=plane[:, t * P : (t + 1) * P],
+                    rhs=v_codes[a][:, cols].bitcast(FP8X4),
+                    rhs_scale=v_planes[4 * a : P, cols],
+                    start=(a == 0),
+                    stop=(a == K_PASSES - 1),
+                )
+
+        def new_banks():
+            return [psum.tile([P, BANK], F32, name="bank") for half in range(2)]
+
+        def features(banks, b, t, products):
+            folded = ring.tile([P, S], F32, name="folded")
+            for half in range(2):
+                nc.scalar.activation(
+                    folded[:, half * BANK : (half + 1) * BANK], banks[half][:], ACT.Abs,
+                    bias=phase_cols[:, b, t : t + 1],
+                )
+            h = ring.tile([P, S], F32, name="h", bufs=4)
+            nc.scalar.activation(h[:], folded[:], ACT.Sin, bias=math.pi / 2, scale=-1.0)
+            left = ring.tile([P, PAIRS], F32, name="left")
+            nc.vector.tensor_tensor(left[:], h[:].indirect(pos1_sb[:]), gain_rows[b][:, t, :], ALU.mult)
+            nc.vector.tensor_tensor(products[:, t, :], h[:].indirect(pos2_sb[:]), left[:], ALU.mult)
+
+        def quantise_z(products, b):
+            rounded_z = held.tile([P, PACK * PAIRS], BF16, name="z_rounded_%d" % b, align_bytes=64)
+            nc.vector.tensor_copy(
+                rounded_z[:].rearrange("p (c i t) -> p c t i", i=4, t=PACK),
+                products[:].rearrange("p t (c i) -> p c t i", i=4),
+            )
+            codes = held.tile([P, PAIRS], U32, name="z_codes_%d" % b, align_bytes=64)
+            plane = held.tile([P, PAIRS], U8, name="z_plane_%d" % b, align_bytes=64)
+            nc.vector.quantize_mx(codes[:].bitcast(FP8X4), plane[:], rounded_z[:])
+            return codes, plane
+
+        z_mx = []
+        for b in range(H_PASSES):
+            group = [new_banks() for t in range(PACK)]
+            for a in range(K_PASSES):
+                for t in range(PACK):
+                    first_pass(group[t], a, b, t)
+            products = held.tile([P, PACK, PAIRS], F32, name="products_%d" % b)
+            for t in range(PACK):
+                features(group[t], b, t, products)
+                if b == 0 and t < K_PASSES:
+                    rounded = new_rounded()
+                    copy = nc.scalar.copy if t == K_PASSES - 1 else nc.vector.tensor_copy
+                    round_w1(copy, rounded, raw_late[t], 0)
+                    w1_mx[t, 1] = quantise_w1(rounded, "w1_%d1" % t, [0, PASS])
+            z_mx.append(quantise_z(products, b))
+
+        y_banks = [psum.tile([P, BANK], F32, name="bank") for i in range(N // P)]
+        for b in range(H_PASSES):
+            codes, plane = z_mx[b]
+            for i in range(N // P):
+                nc.tensor.matmul_mx(
+                    y_banks[i][:],
+                    lhsT=w2_codes[:, b, 2 * i * P : 2 * (i + 1) * P].bitcast(FP4X4),
+                    lhsT_scale=w2_planes[:, b, i * P : (i + 1) * P],
+                    rhs=codes[:].bitcast(FP8X4),
+                    rhs_scale=plane[:],
+                    start=(b == 0),
+                    stop=(b == H_PASSES - 1),
+                )
+        for i in range(N // P):
+            y = held.tile([P, PAIRS], F32, name="y_%d" % i)
+            nc.scalar.copy(y[:], y_banks[i][:])
+            one_side = ring.tile([P, CONTRASTS], F32, name="one_side")
+            nc.vector.tensor_copy(one_side[:], y[:].indirect(pos3_sb[:]))
+            diff = ring.tile([P, CONTRASTS], F32, name="diff")
+            nc.vector.tensor_tensor(diff[:], y[:].indirect(pos4_sb[:]), one_side[:], ALU.subtract)
+            squared = ring.tile([P, CONTRASTS], F32, name="squared", bufs=4)
+            nc.scalar.activation(squared[:], diff[:], ACT.Square)
+            nc.sync.dma_start(out[i * P : (i + 1) * P, :], squared[:])

@@ -23,6 +23,10 @@ PASS = P * PACK
 BANK = 512
 K_PASSES = K // PASS
 H_PASSES = H // PASS
+KIB = 1024
+WORDS_AT = [8 * KIB * a for a in range(K_PASSES)]
+LAST_RAW_AT = 40 * KIB
+FOLDED_AT = [24 * KIB + 4 * KIB * t for t in range(PACK)]
 
 
 def tile_list_echo_chamber_contrast_kernel(
@@ -31,8 +35,12 @@ def tile_list_echo_chamber_contrast_kernel(
     nc = tc.nc
     with ExitStack() as ctx:
         held = ctx.enter_context(tc.tile_pool(name="held", bufs=1))
+        reused = ctx.enter_context(tc.tile_pool(name="reused", bufs=1))
         ring = ctx.enter_context(tc.tile_pool(name="ring", bufs=3))
         psum = ctx.enter_context(tc.psum_pool(name="psum", bufs=8))
+
+        def placed(shape, dtype, name, at):
+            return reused.tile(shape, dtype, name=name, align_bytes=64, offset=at)
 
         def load_list(name, src):
             t = held.tile(list(src.shape), U16, name=name)
@@ -40,44 +48,48 @@ def tile_list_echo_chamber_contrast_kernel(
             return t
 
         def load_table_words(a):
-            t = held.tile([P, T], I32, name="tab_words_%d" % a)
+            t = placed([P, T], I32, "tab_words_%d" % a, WORDS_AT[a])
             nc.sync.dma_start(t[:], tab_words[a].rearrange("p t i -> p (t i)").bitcast(I32))
             return t
 
-        def load_w1(a, c0, c1):
-            t = held.tile([P, PACK, c1 - c0], F32, name="w1_raw_%d_%d" % (a, c0))
+        def load_w1(a, c0, c1, at=None):
+            shape, name = [P, PACK, c1 - c0], "w1_raw_%d_%d" % (a, c0)
+            t = held.tile(shape, F32, name=name) if at is None else placed(shape, F32, name, at)
             rows = w1[a * PASS : (a + 1) * PASS, c0:c1]
             nc.sync.dma_start(t[:], rows.rearrange("(p j) c -> p j c", j=PACK))
             return t
 
         tab_planes = held.tile([P, T], U8, name="tab_planes")
-        nc.gpsimd.memset(tab_planes[:].bitcast(I32), 0)
-        for q in range(4):
-            nc.gpsimd.dma_start(
-                tab_planes[32 * q : 32 * q + 4 * K_PASSES, :].bitcast(I32),
-                tab_scales[:, 4 * q : 4 * q + 4, :].bitcast(I32),
-            )
+        nc.vector.memset(tab_planes[:].bitcast(I32), 0)
         gain_cols = held.tile([P, H_PASSES, PACK], F32, name="gain_cols")
         phase_cols = held.tile([P, H_PASSES, PACK], F32, name="phase_cols")
         nc.scalar.dma_start(gain_cols[:], gain.rearrange("(b p t) -> p b t", b=H_PASSES, t=PACK))
         nc.scalar.dma_start(phase_cols[:], phase.rearrange("(b p t) -> p b t", b=H_PASSES, t=PACK))
+        warm = held.tile([P, 2], F32, name="warm")
+        nc.vector.memset(warm[:, 0:1], 0.0)
+        nc.scalar.activation(warm[:, 1:2], warm[:, 0:1], ACT.Sin)
 
-        words0 = load_table_words(0)
         offs_sb = load_list("offs_sb", offs)
-        raw00 = load_w1(0, 0, PASS)
-        words1 = load_table_words(1)
-        raw10 = load_w1(1, 0, PASS)
-        words2 = load_table_words(2)
-        raw20a = load_w1(2, 0, PASS // 2)
-        raw20b = load_w1(2, PASS // 2, PASS)
         pos1_sb = load_list("pos1_sb", pos1)
         pos2_sb = load_list("pos2_sb", pos2)
+        pos3_sb = load_list("pos3_sb", pos3)
+        words = [load_table_words(0)]
+        raw00 = load_w1(0, 0, PASS)
+        for q in range(4):
+            nc.sync.dma_start(
+                tab_planes[32 * q : 32 * q + 4 * K_PASSES, :].bitcast(I32),
+                tab_scales[:, 4 * q : 4 * q + 4, :].bitcast(I32),
+            )
+        words.append(load_table_words(1))
+        words.append(load_table_words(2))
+        raw10a = load_w1(1, 0, PASS // 2)
+        raw10b = load_w1(1, PASS // 2, PASS)
+        raw20a = load_w1(2, 0, PASS // 2)
+        raw20b = load_w1(2, PASS // 2, PASS, LAST_RAW_AT)
         raw_late = [load_w1(a, PASS, 2 * PASS) for a in range(K_PASSES)]
         w2_codes = held.tile([P, H_PASSES, 2 * N], U8, name="w2_codes", align_bytes=64)
         nc.sync.dma_start(w2_codes[:].bitcast(I32), w2_words.rearrange("b p c -> p b c").bitcast(I32))
-        pos3_sb = load_list("pos3_sb", pos3)
         pos4_sb = load_list("pos4_sb", pos4)
-
         w2_planes = held.tile([P, H_PASSES, N], U8, name="w2_planes", align_bytes=64)
         nc.vector.memset(w2_planes[:].bitcast(I32), 0)
         for q in range(4):
@@ -86,117 +98,138 @@ def tile_list_echo_chamber_contrast_kernel(
                 w2_scales[:, 4 * q : 4 * q + 4, :].rearrange("b r c -> r b c").bitcast(I32),
             )
 
-        gain_rows = []
+        gain_rows = [held.tile([P, PACK, PAIRS], F32, name="gain_rows_%d" % b) for b in range(H_PASSES)]
         for b in range(H_PASSES):
-            g = held.tile([P, PACK, PAIRS], F32, name="gain_rows_%d" % b)
-            gain_rows.append(g)
-
-        def spread_gain(b):
             nc.scalar.copy(gain_rows[b][:], gain_cols[:, b, :].unsqueeze(2).to_broadcast([P, PACK, PAIRS]))
 
-        def gather_words(window, a):
+        def gather_words(a):
             t = held.tile([P, S], U32, name="v_codes_%d" % a, align_bytes=64)
-            nc.vector.tensor_copy(t[:], window[:].bitcast(U32).indirect(offs_sb[:]))
+            nc.vector.tensor_copy(t[:], words[a][:].bitcast(U32).indirect(offs_sb[:]))
             return t
-
-        def new_rounded():
-            return ring.tile([P, PACK * PASS], BF16, name="w1_rounded", align_bytes=64)
 
         def round_w1(copy, rounded, raw, m0):
             m1 = m0 + raw.shape[2] // PACK
             dst = rounded[:].rearrange("p (t m j) -> p m j t", t=PACK, j=PACK)
             copy(dst[:, m0:m1, :, :], raw[:].rearrange("p j (m t) -> p m j t", t=PACK))
 
-        def quantise_w1(rounded, name, cuts):
-            codes = held.tile([P, PASS], U32, name=name + "_codes", align_bytes=64)
-            plane = held.tile([P, PASS], U8, name=name + "_plane", align_bytes=64)
-            for c0, c1 in zip(cuts[:-1], cuts[1:]):
-                nc.vector.quantize_mx(
-                    codes[:, c0:c1].bitcast(FP8X4), plane[:, c0:c1], rounded[:, PACK * c0 : PACK * c1]
-                )
-            return codes, plane
+        w1_planes = {
+            (a, b): held.tile([P, PASS], U8, name="w1_plane_%d%d" % (a, b), align_bytes=64)
+            for a in range(K_PASSES)
+            for b in range(H_PASSES)
+        }
+        w1_codes = {}
 
-        v_codes = [None] * K_PASSES
-        w1_mx = {}
-        spread_gain(0)
-        v_codes[0] = gather_words(words0, 0)
+        def quantise_w1(a, b, rounded, t0, t1, at=None):
+            shape, name = [P, (t1 - t0) * P], "w1_codes_%d%d%d" % (a, b, t0)
+            if at is None:
+                codes = held.tile(shape, U32, name=name, align_bytes=64)
+            else:
+                codes = placed(shape, U32, name, at)
+            nc.vector.quantize_mx(
+                codes[:].bitcast(FP8X4), w1_planes[a, b][:, t0 * P : t1 * P], rounded[:, t0 * PASS : t1 * PASS]
+            )
+            for t in range(t0, t1):
+                w1_codes[a, b, t] = codes[:, (t - t0) * P : (t - t0 + 1) * P]
+
+        v_codes = [gather_words(0)]
         v_planes = held.tile([P, S], U8, name="v_planes", align_bytes=64)
         nc.vector.tensor_copy(v_planes[:], tab_planes[:].indirect(offs_sb[:]))
-        rounded = new_rounded()
-        round_w1(nc.scalar.copy, rounded, raw00, 0)
-        spread_gain(1)
-        v_codes[1] = gather_words(words1, 1)
-        w1_mx[0, 0] = quantise_w1(rounded, "w1_00", [0, PASS])
-        rounded = new_rounded()
-        round_w1(nc.scalar.copy, rounded, raw10, 0)
-        v_codes[2] = gather_words(words2, 2)
-        w1_mx[1, 0] = quantise_w1(rounded, "w1_10", [0, PASS])
-        rounded = new_rounded()
-        round_w1(nc.scalar.copy, rounded, raw20a, 0)
-        round_w1(nc.vector.tensor_copy, rounded, raw20b, P // 2)
-        w1_mx[2, 0] = quantise_w1(rounded, "w1_20", [0, P, 2 * P, PASS])
+        v_codes.append(gather_words(1))
+        rounded0 = held.tile([P, PACK * PASS], BF16, name="rounded0", align_bytes=64)
+        round_w1(nc.scalar.copy, rounded0, raw00, 0)
+        quantise_w1(0, 0, rounded0, 0, PACK, WORDS_AT[1])
+        v_codes.append(gather_words(2))
+        rounded1 = held.tile([P, PACK * PASS], BF16, name="rounded1", align_bytes=64)
+        round_w1(nc.scalar.copy, rounded1, raw10a, 0)
+        round_w1(nc.scalar.copy, rounded1, raw10b, P // 2)
+        rounded2 = placed([P, PACK * PASS], BF16, "rounded2", WORDS_AT[2])
+        round_w1(nc.vector.tensor_copy, rounded2, raw20a, 0)
+        quantise_w1(1, 0, rounded1, 0, 1, WORDS_AT[2] + 4 * KIB)
+        round_w1(nc.vector.tensor_copy, rounded2, raw20b, P // 2)
+        quantise_w1(2, 0, rounded2, 0, 1)
+        quantise_w1(1, 0, rounded1, 1, 2, LAST_RAW_AT)
+        quantise_w1(2, 0, rounded2, 1, 2)
+        quantise_w1(1, 0, rounded1, 2, PACK, LAST_RAW_AT + KIB)
+        quantise_w1(2, 0, rounded2, 2, PACK)
+        rounded_late0 = placed([P, PACK * PASS], BF16, "rounded_late0", WORDS_AT[2])
+        round_w1(nc.vector.tensor_copy, rounded_late0, raw_late[0], 0)
+        quantise_w1(0, 1, rounded_late0, 0, PACK)
 
-        def first_pass(banks, a, b, t):
-            codes, plane = w1_mx[a, b]
+        def first_product(b, t):
+            banks = [psum.tile([P, BANK], F32, name="bank") for half in range(2)]
+            for a in range(K_PASSES):
+                for half in range(2):
+                    cols = slice(half * BANK, (half + 1) * BANK)
+                    nc.tensor.matmul_mx(
+                        banks[half][:],
+                        lhsT=w1_codes[a, b, t].bitcast(FP8X4),
+                        lhsT_scale=w1_planes[a, b][:, t * P : (t + 1) * P],
+                        rhs=v_codes[a][:, cols].bitcast(FP8X4),
+                        rhs_scale=v_planes[4 * a : P, cols],
+                        start=(a == 0),
+                        stop=(a == K_PASSES - 1),
+                    )
+            return banks
+
+        def cosine(banks, b, t):
+            folded = placed([P, S], F32, "folded_%d%d" % (b, t), FOLDED_AT[t])
+            h = ring.tile([P, S], F32, name="h", bufs=4)
             for half in range(2):
                 cols = slice(half * BANK, (half + 1) * BANK)
-                nc.tensor.matmul_mx(
-                    banks[half][:],
-                    lhsT=codes[:, t * P : (t + 1) * P].bitcast(FP8X4),
-                    lhsT_scale=plane[:, t * P : (t + 1) * P],
-                    rhs=v_codes[a][:, cols].bitcast(FP8X4),
-                    rhs_scale=v_planes[4 * a : P, cols],
-                    start=(a == 0),
-                    stop=(a == K_PASSES - 1),
-                )
-
-        def new_banks():
-            return [psum.tile([P, BANK], F32, name="bank") for half in range(2)]
-
-        def features(banks, b, t, products):
-            folded = ring.tile([P, S], F32, name="folded")
+                nc.scalar.activation(folded[:, cols], banks[half][:], ACT.Abs, bias=phase_cols[:, b, t : t + 1])
             for half in range(2):
-                nc.scalar.activation(
-                    folded[:, half * BANK : (half + 1) * BANK], banks[half][:], ACT.Abs,
-                    bias=phase_cols[:, b, t : t + 1],
-                )
-            h = ring.tile([P, S], F32, name="h", bufs=4)
-            nc.scalar.activation(h[:], folded[:], ACT.Sin, bias=math.pi / 2, scale=-1.0)
-            left = ring.tile([P, PAIRS], F32, name="left")
-            nc.vector.tensor_tensor(left[:], h[:].indirect(pos1_sb[:]), gain_rows[b][:, t, :], ALU.mult)
-            nc.vector.tensor_tensor(products[:, t, :], h[:].indirect(pos2_sb[:]), left[:], ALU.mult)
+                cols = slice(half * BANK, (half + 1) * BANK)
+                nc.scalar.activation(h[:, cols], folded[:, cols], ACT.Sin, bias=math.pi / 2, scale=-1.0)
+            return h
 
-        def quantise_z(products, b):
-            rounded_z = held.tile([P, PACK * PAIRS], BF16, name="z_rounded_%d" % b, align_bytes=64)
-            nc.vector.tensor_copy(
+        def pair_products(h, b, t, products):
+            left = ring.tile([P, PAIRS], F32, name="left")
+            width = PAIRS // 1
+            for m0 in range(0, PAIRS, width):
+                picks = pos1_sb[:, m0 // 16 : (m0 + width) // 16]
+                nc.vector.tensor_tensor(
+                    left[:, m0 : m0 + width], h[:].indirect(picks), gain_rows[b][:, t, m0 : m0 + width], ALU.mult
+                )
+            for m0 in range(0, PAIRS, width):
+                picks = pos2_sb[:, m0 // 16 : (m0 + width) // 16]
+                nc.vector.tensor_tensor(
+                    products[:, t, m0 : m0 + width], h[:].indirect(picks), left[:, m0 : m0 + width], ALU.mult
+                )
+
+        def round_z(copy, rounded_z, products):
+            copy(
                 rounded_z[:].rearrange("p (c i t) -> p c t i", i=4, t=PACK),
                 products[:].rearrange("p t (c i) -> p c t i", i=4),
             )
+
+        def quantise_z(rounded_z, b):
             codes = held.tile([P, PAIRS], U32, name="z_codes_%d" % b, align_bytes=64)
             plane = held.tile([P, PAIRS], U8, name="z_plane_%d" % b, align_bytes=64)
             nc.vector.quantize_mx(codes[:].bitcast(FP8X4), plane[:], rounded_z[:])
             return codes, plane
 
-        z_mx = []
+        products = [held.tile([P, PACK, PAIRS], F32, name="products_%d" % b) for b in range(H_PASSES)]
+        late_rounding = {0: (1, nc.vector.tensor_copy), 2: (2, nc.scalar.copy)}
         for b in range(H_PASSES):
-            group = [new_banks() for t in range(PACK)]
-            for a in range(K_PASSES):
-                for t in range(PACK):
-                    first_pass(group[t], a, b, t)
-            products = held.tile([P, PACK, PAIRS], F32, name="products_%d" % b)
             for t in range(PACK):
-                features(group[t], b, t, products)
-                if b == 0 and t < K_PASSES:
-                    rounded = new_rounded()
-                    copy = nc.scalar.copy if t == K_PASSES - 1 else nc.vector.tensor_copy
-                    round_w1(copy, rounded, raw_late[t], 0)
-                    w1_mx[t, 1] = quantise_w1(rounded, "w1_%d1" % t, [0, PASS])
-            z_mx.append(quantise_z(products, b))
+                h = cosine(first_product(b, t), b, t)
+                pair_products(h, b, t, products[b])
+                if b == 0 and t in late_rounding:
+                    a, copy = late_rounding[t]
+                    rounded = placed([P, PACK * PASS], BF16, "rounded_late%d" % a, FOLDED_AT[t])
+                    round_w1(copy, rounded, raw_late[a], 0)
+                    quantise_w1(a, 1, rounded, 0, PACK)
+
+        rounded_z0 = placed([P, PACK * PAIRS], BF16, "rounded_z0", FOLDED_AT[PACK - 1])
+        round_z(nc.scalar.copy, rounded_z0, products[0])
+        rounded_z1 = held.tile([P, PACK * PAIRS], BF16, name="rounded_z1", align_bytes=64)
+        round_z(nc.vector.tensor_copy, rounded_z1, products[1])
+        z_mx = [quantise_z(rounded_z0, 0), quantise_z(rounded_z1, 1)]
 
         y_banks = [psum.tile([P, BANK], F32, name="bank") for i in range(N // P)]
-        for b in range(H_PASSES):
-            codes, plane = z_mx[b]
-            for i in range(N // P):
+        for i in range(N // P):
+            for b in range(H_PASSES):
+                codes, plane = z_mx[b]
                 nc.tensor.matmul_mx(
                     y_banks[i][:],
                     lhsT=w2_codes[:, b, 2 * i * P : 2 * (i + 1) * P].bitcast(FP4X4),

@@ -25,8 +25,10 @@ K_PASSES = K // PASS
 H_PASSES = H // PASS
 KIB = 1024
 WORDS_AT = [8 * KIB * a for a in range(K_PASSES)]
+VECTOR_SHARE = 84
 LAST_RAW_AT = 40 * KIB
-FOLDED_AT = [24 * KIB + 4 * KIB * t for t in range(PACK)]
+FOLDED_AT = [[24 * KIB, 26 * KIB, 32 * KIB, 36 * KIB], [24 * KIB, 28 * KIB, 32 * KIB, 36 * KIB]]
+LATE_AT = {2: 26 * KIB}
 
 
 def tile_list_echo_chamber_contrast_kernel(
@@ -70,9 +72,6 @@ def tile_list_echo_chamber_contrast_kernel(
         nc.scalar.activation(warm[:, 1:2], warm[:, 0:1], ACT.Sin)
 
         offs_sb = load_list("offs_sb", offs)
-        pos1_sb = load_list("pos1_sb", pos1)
-        pos2_sb = load_list("pos2_sb", pos2)
-        pos3_sb = load_list("pos3_sb", pos3)
         words = [load_table_words(0)]
         raw00 = load_w1(0, 0, PASS)
         for q in range(4):
@@ -82,13 +81,14 @@ def tile_list_echo_chamber_contrast_kernel(
             )
         words.append(load_table_words(1))
         words.append(load_table_words(2))
-        raw10a = load_w1(1, 0, PASS // 2)
-        raw10b = load_w1(1, PASS // 2, PASS)
-        raw20a = load_w1(2, 0, PASS // 2)
-        raw20b = load_w1(2, PASS // 2, PASS, LAST_RAW_AT)
+        raw10 = load_w1(1, 0, PASS)
+        raw20 = load_w1(2, 0, PASS, LAST_RAW_AT)
+        pos1_sb = load_list("pos1_sb", pos1)
+        pos2_sb = load_list("pos2_sb", pos2)
         raw_late = [load_w1(a, PASS, 2 * PASS) for a in range(K_PASSES)]
         w2_codes = held.tile([P, H_PASSES, 2 * N], U8, name="w2_codes", align_bytes=64)
         nc.sync.dma_start(w2_codes[:].bitcast(I32), w2_words.rearrange("b p c -> p b c").bitcast(I32))
+        pos3_sb = load_list("pos3_sb", pos3)
         pos4_sb = load_list("pos4_sb", pos4)
         w2_planes = held.tile([P, H_PASSES, N], U8, name="w2_planes", align_bytes=64)
         nc.vector.memset(w2_planes[:].bitcast(I32), 0)
@@ -107,10 +107,10 @@ def tile_list_echo_chamber_contrast_kernel(
             nc.vector.tensor_copy(t[:], words[a][:].bitcast(U32).indirect(offs_sb[:]))
             return t
 
-        def round_w1(copy, rounded, raw, m0):
-            m1 = m0 + raw.shape[2] // PACK
+        def round_w1(copy, rounded, raw, m0=0, m1=P):
             dst = rounded[:].rearrange("p (t m j) -> p m j t", t=PACK, j=PACK)
-            copy(dst[:, m0:m1, :, :], raw[:].rearrange("p j (m t) -> p m j t", t=PACK))
+            src = raw[:].rearrange("p j (m t) -> p m j t", t=PACK)
+            copy(dst[:, m0:m1, :, :], src[:, m0:m1, :, :])
 
         w1_planes = {
             (a, b): held.tile([P, PASS], U8, name="w1_plane_%d%d" % (a, b), align_bytes=64)
@@ -136,29 +136,29 @@ def tile_list_echo_chamber_contrast_kernel(
         nc.vector.tensor_copy(v_planes[:], tab_planes[:].indirect(offs_sb[:]))
         v_codes.append(gather_words(1))
         rounded0 = held.tile([P, PACK * PASS], BF16, name="rounded0", align_bytes=64)
-        round_w1(nc.scalar.copy, rounded0, raw00, 0)
+        round_w1(nc.scalar.copy, rounded0, raw00)
         quantise_w1(0, 0, rounded0, 0, PACK, WORDS_AT[1])
         v_codes.append(gather_words(2))
         rounded1 = held.tile([P, PACK * PASS], BF16, name="rounded1", align_bytes=64)
-        round_w1(nc.scalar.copy, rounded1, raw10a, 0)
-        round_w1(nc.scalar.copy, rounded1, raw10b, P // 2)
+        round_w1(nc.scalar.copy, rounded1, raw10)
         rounded2 = placed([P, PACK * PASS], BF16, "rounded2", WORDS_AT[2])
-        round_w1(nc.vector.tensor_copy, rounded2, raw20a, 0)
-        quantise_w1(1, 0, rounded1, 0, 1, WORDS_AT[2] + 4 * KIB)
-        round_w1(nc.vector.tensor_copy, rounded2, raw20b, P // 2)
+        round_w1(nc.vector.tensor_copy, rounded2, raw20, 0, VECTOR_SHARE)
+        round_w1(nc.scalar.copy, rounded2, raw20, VECTOR_SHARE, P)
+        quantise_w1(1, 0, rounded1, 0, 1, LAST_RAW_AT)
         quantise_w1(2, 0, rounded2, 0, 1)
-        quantise_w1(1, 0, rounded1, 1, 2, LAST_RAW_AT)
+        quantise_w1(1, 0, rounded1, 1, 2, LAST_RAW_AT + KIB)
         quantise_w1(2, 0, rounded2, 1, 2)
-        quantise_w1(1, 0, rounded1, 2, PACK, LAST_RAW_AT + KIB)
+        quantise_w1(1, 0, rounded1, 2, PACK, LAST_RAW_AT + 2 * KIB)
         quantise_w1(2, 0, rounded2, 2, PACK)
-        rounded_late0 = placed([P, PACK * PASS], BF16, "rounded_late0", WORDS_AT[2])
-        round_w1(nc.vector.tensor_copy, rounded_late0, raw_late[0], 0)
-        quantise_w1(0, 1, rounded_late0, 0, PACK)
+        for a in range(K_PASSES - 1):
+            rounded = placed([P, PACK * PASS], BF16, "rounded_late%d" % a, WORDS_AT[2])
+            round_w1(nc.vector.tensor_copy, rounded, raw_late[a])
+            quantise_w1(a, 1, rounded, 0, PACK)
 
         def first_product(b, t):
             banks = [psum.tile([P, BANK], F32, name="bank") for half in range(2)]
-            for a in range(K_PASSES):
-                for half in range(2):
+            for half in range(2):
+                for a in range(K_PASSES):
                     cols = slice(half * BANK, (half + 1) * BANK)
                     nc.tensor.matmul_mx(
                         banks[half][:],
@@ -172,7 +172,7 @@ def tile_list_echo_chamber_contrast_kernel(
             return banks
 
         def cosine(banks, b, t):
-            folded = placed([P, S], F32, "folded_%d%d" % (b, t), FOLDED_AT[t])
+            folded = placed([P, S], F32, "folded_%d%d" % (b, t), FOLDED_AT[b][t])
             h = ring.tile([P, S], F32, name="h", bufs=4)
             for half in range(2):
                 cols = slice(half * BANK, (half + 1) * BANK)
@@ -184,7 +184,7 @@ def tile_list_echo_chamber_contrast_kernel(
 
         def pair_products(h, b, t, products):
             left = ring.tile([P, PAIRS], F32, name="left")
-            width = PAIRS // 1
+            width = PAIRS // 2
             for m0 in range(0, PAIRS, width):
                 picks = pos1_sb[:, m0 // 16 : (m0 + width) // 16]
                 nc.vector.tensor_tensor(
@@ -196,56 +196,74 @@ def tile_list_echo_chamber_contrast_kernel(
                     products[:, t, m0 : m0 + width], h[:].indirect(picks), left[:, m0 : m0 + width], ALU.mult
                 )
 
-        def round_z(copy, rounded_z, products):
+        z_codes = [held.tile([P, PAIRS], U32, name="z_codes_%d" % b, align_bytes=64) for b in range(H_PASSES)]
+        z_planes = [held.tile([P, PAIRS], U8, name="z_plane_%d" % b, align_bytes=64) for b in range(H_PASSES)]
+
+        def round_z(copy, rounded_z, b, m0, m1):
             copy(
-                rounded_z[:].rearrange("p (c i t) -> p c t i", i=4, t=PACK),
-                products[:].rearrange("p t (c i) -> p c t i", i=4),
+                rounded_z.rearrange("p (c i t) -> p c t i", i=4, t=PACK),
+                products[b][:, :, m0:m1].rearrange("p t (c i) -> p c t i", i=4),
             )
 
-        def quantise_z(rounded_z, b):
-            codes = held.tile([P, PAIRS], U32, name="z_codes_%d" % b, align_bytes=64)
-            plane = held.tile([P, PAIRS], U8, name="z_plane_%d" % b, align_bytes=64)
-            nc.vector.quantize_mx(codes[:].bitcast(FP8X4), plane[:], rounded_z[:])
-            return codes, plane
+        def quantise_z(rounded_z, b, m0, m1):
+            nc.vector.quantize_mx(z_codes[b][:, m0:m1].bitcast(FP8X4), z_planes[b][:, m0:m1], rounded_z)
 
         products = [held.tile([P, PACK, PAIRS], F32, name="products_%d" % b) for b in range(H_PASSES)]
-        late_rounding = {0: (1, nc.vector.tensor_copy), 2: (2, nc.scalar.copy)}
+        late_rounding = {1: (2, nc.scalar.copy)}
         for b in range(H_PASSES):
             for t in range(PACK):
                 h = cosine(first_product(b, t), b, t)
                 pair_products(h, b, t, products[b])
                 if b == 0 and t in late_rounding:
                     a, copy = late_rounding[t]
-                    rounded = placed([P, PACK * PASS], BF16, "rounded_late%d" % a, FOLDED_AT[t])
-                    round_w1(copy, rounded, raw_late[a], 0)
+                    rounded = placed([P, PACK * PASS], BF16, "rounded_late%d" % a, LATE_AT[a])
+                    round_w1(copy, rounded, raw_late[a])
                     quantise_w1(a, 1, rounded, 0, PACK)
+                if (b, t) == (0, PACK - 1):
+                    rounded = held.tile([P, PACK * PAIRS // 2], BF16, name="rounded_z0_low", align_bytes=64)
+                    round_z(nc.vector.tensor_copy, rounded[:], 0, 0, PAIRS // 2)
+                    quantise_z(rounded[:], 0, 0, PAIRS // 2)
+                if (b, t) == (1, PACK - 2):
+                    rounded = placed([P, PACK * PAIRS // 2], BF16, "rounded_z0_high", FOLDED_AT[b][t] + 2 * KIB)
+                    round_z(nc.scalar.copy, rounded[:], 0, PAIRS // 2, PAIRS)
+                    quantise_z(rounded[:], 0, PAIRS // 2, PAIRS)
 
-        rounded_z0 = placed([P, PACK * PAIRS], BF16, "rounded_z0", FOLDED_AT[PACK - 1])
-        round_z(nc.scalar.copy, rounded_z0, products[0])
         rounded_z1 = held.tile([P, PACK * PAIRS], BF16, name="rounded_z1", align_bytes=64)
-        round_z(nc.vector.tensor_copy, rounded_z1, products[1])
-        z_mx = [quantise_z(rounded_z0, 0), quantise_z(rounded_z1, 1)]
+        round_z(nc.scalar.copy, rounded_z1[:, 0 : PACK * PAIRS // 2], 1, 0, PAIRS // 2)
+        round_z(nc.vector.tensor_copy, rounded_z1[:, PACK * PAIRS // 2 : PACK * PAIRS], 1, PAIRS // 2, PAIRS)
+        quantise_z(rounded_z1[:, 0 : PACK * PAIRS // 2], 1, 0, PAIRS // 2)
+        quantise_z(rounded_z1[:, PACK * PAIRS // 2 : PACK * PAIRS], 1, PAIRS // 2, PAIRS)
 
         y_banks = [psum.tile([P, BANK], F32, name="bank") for i in range(N // P)]
         for i in range(N // P):
             for b in range(H_PASSES):
-                codes, plane = z_mx[b]
-                nc.tensor.matmul_mx(
-                    y_banks[i][:],
-                    lhsT=w2_codes[:, b, 2 * i * P : 2 * (i + 1) * P].bitcast(FP4X4),
-                    lhsT_scale=w2_planes[:, b, i * P : (i + 1) * P],
-                    rhs=codes[:].bitcast(FP8X4),
-                    rhs_scale=plane[:],
-                    start=(b == 0),
-                    stop=(b == H_PASSES - 1),
-                )
+                width = P if (i, b) == (0, H_PASSES - 1) else PAIRS
+                for m0 in range(0, PAIRS, width):
+                    nc.tensor.matmul_mx(
+                        y_banks[i][:, m0 : m0 + width],
+                        lhsT=w2_codes[:, b, 2 * i * P : 2 * (i + 1) * P].bitcast(FP4X4),
+                        lhsT_scale=w2_planes[:, b, i * P : (i + 1) * P],
+                        rhs=z_codes[b][:, m0 : m0 + width].bitcast(FP8X4),
+                        rhs_scale=z_planes[b][:, m0 : m0 + width],
+                        start=(b == 0),
+                        stop=(b == H_PASSES - 1 and m0 + width == PAIRS),
+                    )
+        y_rows = [held.tile([P, PAIRS], F32, name="y_%d" % i) for i in range(N // P)]
         for i in range(N // P):
-            y = held.tile([P, PAIRS], F32, name="y_%d" % i)
-            nc.scalar.copy(y[:], y_banks[i][:])
+            nc.scalar.copy(y_rows[i][:], y_banks[i][:])
+        for i in range(N // P):
             one_side = ring.tile([P, CONTRASTS], F32, name="one_side")
-            nc.vector.tensor_copy(one_side[:], y[:].indirect(pos3_sb[:]))
             diff = ring.tile([P, CONTRASTS], F32, name="diff")
-            nc.vector.tensor_tensor(diff[:], y[:].indirect(pos4_sb[:]), one_side[:], ALU.subtract)
+            width = CONTRASTS
+            for j0 in range(0, CONTRASTS, width):
+                picks = pos3_sb[:, j0 // 16 : (j0 + width) // 16]
+                nc.vector.tensor_copy(one_side[:, j0 : j0 + width], y_rows[i][:].indirect(picks))
+            for j0 in range(0, CONTRASTS, width):
+                picks = pos4_sb[:, j0 // 16 : (j0 + width) // 16]
+                nc.vector.tensor_tensor(
+                    diff[:, j0 : j0 + width], y_rows[i][:].indirect(picks), one_side[:, j0 : j0 + width], ALU.subtract
+                )
             squared = ring.tile([P, CONTRASTS], F32, name="squared", bufs=4)
             nc.scalar.activation(squared[:], diff[:], ACT.Square)
-            nc.sync.dma_start(out[i * P : (i + 1) * P, :], squared[:])
+            queue = nc.scalar if i == N // P - 1 else nc.sync
+            queue.dma_start(out[i * P : (i + 1) * P, :], squared[:])

@@ -18,17 +18,30 @@ ACT = mybir.ActivationFunctionType
 ALU = mybir.AluOpType
 
 P = 128
+HALF_P = P // 2
 PACK = 4
 PASS = P * PACK
 BANK = 512
 K_PASSES = K // PASS
 H_PASSES = H // PASS
 KIB = 1024
-WORDS_AT = [8 * KIB * a for a in range(K_PASSES)]
-VECTOR_SHARE = 84
-LAST_RAW_AT = 40 * KIB
-FOLDED_AT = [[24 * KIB, 26 * KIB, 32 * KIB, 36 * KIB], [24 * KIB, 28 * KIB, 32 * KIB, 36 * KIB]]
-LATE_AT = {2: 26 * KIB}
+HALF = PAIRS // 2
+QUARTER = PAIRS // 4
+COLUMN_GROUPS = [(0, 256), (256, 512), (512, 1024)]
+SLICES = [(0, 0), (0, 1), (1, 0), (1, 1), (2, 0), (2, 1), (2, 2), (2, 3)]
+EARLY_RAW_AT = 2 * KIB
+LATE_RAW_AT = [8 * KIB, 16 * KIB, 34 * KIB]
+LEFT_LOW_AT = 28 * KIB
+ROUNDED_AT = {
+    (2, 1, 0): LEFT_LOW_AT,
+    (0, 2, 0): EARLY_RAW_AT - 2 * KIB,
+    (1, 2, 0): LEFT_LOW_AT - KIB - KIB // 2,
+    (1, 2, 2): LATE_RAW_AT[0],
+    (2, 2, 0): LEFT_LOW_AT + KIB + KIB // 2,
+    (2, 2, 2): LATE_RAW_AT[1],
+}
+FOLDED_AT = [EARLY_RAW_AT] * 2 + [LATE_RAW_AT[0]] + [LATE_RAW_AT[1]] + [LATE_RAW_AT[2]] * 4
+ROUNDED_Z_AT = {(0, 0): LATE_RAW_AT[2] - 2 * KIB}
 
 
 def tile_list_echo_chamber_contrast_kernel(
@@ -50,42 +63,58 @@ def tile_list_echo_chamber_contrast_kernel(
             return t
 
         def load_table_words(a):
-            t = placed([P, T], I32, "tab_words_%d" % a, WORDS_AT[a])
+            t = held.tile([P, T], I32, name="tab_words_%d" % a)
             nc.sync.dma_start(t[:], tab_words[a].rearrange("p t i -> p (t i)").bitcast(I32))
             return t
 
-        def load_w1(a, c0, c1, at=None):
-            shape, name = [P, PACK, c1 - c0], "w1_raw_%d_%d" % (a, c0)
+        def load_w1(a, g, at=None):
+            c0, c1 = COLUMN_GROUPS[g]
+            shape, name = [P, PACK, c1 - c0], "w1_raw_%d_%d" % (a, g)
             t = held.tile(shape, F32, name=name) if at is None else placed(shape, F32, name, at)
             rows = w1[a * PASS : (a + 1) * PASS, c0:c1]
             nc.sync.dma_start(t[:], rows.rearrange("(p j) c -> p j c", j=PACK))
             return t
 
+        def load_folded_columns(name, vec):
+            t = held.tile([P, 2, 3], F32, name=name)
+            rows = vec[0:PASS].rearrange("(g j t) -> j g t", g=2, t=PACK)
+            nc.scalar.dma_start(t[0:HALF_P, :, :], rows[:, :, 0:3])
+            nc.scalar.dma_start(t[HALF_P:P, :, :], rows[:, :, 1:4])
+            return t
+
+        def load_plain_columns(queue, name, vec):
+            t = held.tile([P, PACK], F32, name=name)
+            queue.dma_start(t[:], vec[PASS : 2 * PASS].rearrange("(p t) -> p t", t=PACK))
+            return t
+
         tab_planes = held.tile([P, T], U8, name="tab_planes")
         nc.vector.memset(tab_planes[:].bitcast(I32), 0)
-        gain_cols = held.tile([P, H_PASSES, PACK], F32, name="gain_cols")
-        phase_cols = held.tile([P, H_PASSES, PACK], F32, name="phase_cols")
-        nc.scalar.dma_start(gain_cols[:], gain.rearrange("(b p t) -> p b t", b=H_PASSES, t=PACK))
-        nc.scalar.dma_start(phase_cols[:], phase.rearrange("(b p t) -> p b t", b=H_PASSES, t=PACK))
+        gain_folded = load_folded_columns("gain_folded", gain)
+        gain_plain = load_plain_columns(nc.scalar, "gain_plain", gain)
+        phase_folded = load_folded_columns("phase_folded", phase)
         warm = held.tile([P, 2], F32, name="warm")
         nc.vector.memset(warm[:, 0:1], 0.0)
         nc.scalar.activation(warm[:, 1:2], warm[:, 0:1], ACT.Sin)
 
         offs_sb = load_list("offs_sb", offs)
-        words = [load_table_words(0)]
-        raw00 = load_w1(0, 0, PASS)
+        words = [load_table_words(0), load_table_words(1)]
+        raw = {(0, 0): load_w1(0, 0)}
         for q in range(4):
             nc.sync.dma_start(
                 tab_planes[32 * q : 32 * q + 4 * K_PASSES, :].bitcast(I32),
                 tab_scales[:, 4 * q : 4 * q + 4, :].bitcast(I32),
             )
-        words.append(load_table_words(1))
+        raw[1, 0] = load_w1(1, 0)
+        raw[2, 0] = load_w1(2, 0)
         words.append(load_table_words(2))
-        raw10 = load_w1(1, 0, PASS)
-        raw20 = load_w1(2, 0, PASS, LAST_RAW_AT)
+        raw[0, 1] = load_w1(0, 1, EARLY_RAW_AT)
+        raw[1, 1] = load_w1(1, 1)
+        raw[2, 1] = load_w1(2, 1)
         pos1_sb = load_list("pos1_sb", pos1)
         pos2_sb = load_list("pos2_sb", pos2)
-        raw_late = [load_w1(a, PASS, 2 * PASS) for a in range(K_PASSES)]
+        phase_plain = load_plain_columns(nc.sync, "phase_plain", phase)
+        for a in range(K_PASSES):
+            raw[a, 2] = load_w1(a, 2, LATE_RAW_AT[a])
         w2_codes = held.tile([P, H_PASSES, 2 * N], U8, name="w2_codes", align_bytes=64)
         nc.sync.dma_start(w2_codes[:].bitcast(I32), w2_words.rearrange("b p c -> p b c").bitcast(I32))
         pos3_sb = load_list("pos3_sb", pos3)
@@ -98,171 +127,185 @@ def tile_list_echo_chamber_contrast_kernel(
                 w2_scales[:, 4 * q : 4 * q + 4, :].rearrange("b r c -> r b c").bitcast(I32),
             )
 
-        gain_rows = [held.tile([P, PACK, PAIRS], F32, name="gain_rows_%d" % b) for b in range(H_PASSES)]
-        for b in range(H_PASSES):
-            nc.scalar.copy(gain_rows[b][:], gain_cols[:, b, :].unsqueeze(2).to_broadcast([P, PACK, PAIRS]))
+        gain_rows = held.tile([P, len(SLICES), HALF], F32, name="gain_rows")
+        nc.scalar.copy(
+            gain_rows[:, 0:4, :].rearrange("p (g u) m -> p g u m", g=2),
+            gain_folded[:, :, 0:3:2].unsqueeze(3).to_broadcast([P, 2, 2, HALF]),
+        )
+        nc.scalar.copy(gain_rows[:, 4:8, :], gain_plain[:].unsqueeze(2).to_broadcast([P, PACK, HALF]))
 
-        def gather_words(a):
-            t = held.tile([P, S], U32, name="v_codes_%d" % a, align_bytes=64)
-            nc.vector.tensor_copy(t[:], words[a][:].bitcast(U32).indirect(offs_sb[:]))
+        def phase_column(s):
+            g, u = SLICES[s]
+            return phase_folded[:, g, 2 * u : 2 * u + 1] if g < 2 else phase_plain[:, u : u + 1]
+
+        def gather_words(a, j0, j1):
+            t = held.tile([P, j1 - j0], U32, name="v_codes_%d_%d" % (a, j0), align_bytes=64)
+            nc.vector.tensor_copy(t[:], words[a][:].bitcast(U32).indirect(offs_sb[:, j0 // 16 : j1 // 16]))
             return t
 
-        def round_w1(copy, rounded, raw, m0=0, m1=P):
-            dst = rounded[:].rearrange("p (t m j) -> p m j t", t=PACK, j=PACK)
-            src = raw[:].rearrange("p j (m t) -> p m j t", t=PACK)
-            copy(dst[:, m0:m1, :, :], src[:, m0:m1, :, :])
+        rounded, w1_codes, w1_planes = {}, {}, {}
 
-        w1_planes = {
-            (a, b): held.tile([P, PASS], U8, name="w1_plane_%d%d" % (a, b), align_bytes=64)
-            for a in range(K_PASSES)
-            for b in range(H_PASSES)
-        }
-        w1_codes = {}
-
-        def quantise_w1(a, b, rounded, t0, t1, at=None):
-            shape, name = [P, (t1 - t0) * P], "w1_codes_%d%d%d" % (a, b, t0)
-            if at is None:
-                codes = held.tile(shape, U32, name=name, align_bytes=64)
+        def round_w1(copy, a, g, t0=0, t1=PACK):
+            c0, c1 = COLUMN_GROUPS[g]
+            shape, name = [P, (t1 - t0) * (c1 - c0)], "rounded_%d%d%d" % (a, g, t0)
+            if (a, g, t0) in ROUNDED_AT:
+                rounded[a, g, t0] = placed(shape, BF16, name, ROUNDED_AT[a, g, t0])
             else:
-                codes = placed(shape, U32, name, at)
-            nc.vector.quantize_mx(
-                codes[:].bitcast(FP8X4), w1_planes[a, b][:, t0 * P : t1 * P], rounded[:, t0 * PASS : t1 * PASS]
+                rounded[a, g, t0] = held.tile(shape, BF16, name=name, align_bytes=64)
+            copy(
+                rounded[a, g, t0][:].rearrange("p (t m j) -> p m j t", t=t1 - t0, j=PACK),
+                raw[a, g][:].rearrange("p j (m t) -> p m j t", t=PACK)[:, :, :, t0:t1],
             )
-            for t in range(t0, t1):
-                w1_codes[a, b, t] = codes[:, (t - t0) * P : (t - t0 + 1) * P]
 
-        v_codes = [gather_words(0)]
+        def quantise_w1(a, g, t0=0, t1=PACK):
+            c0, c1 = COLUMN_GROUPS[g]
+            width = (t1 - t0) * (c1 - c0) // PACK
+            codes = held.tile([P, width], U32, name="w1_codes_%d%d%d" % (a, g, t0), align_bytes=64)
+            plane = held.tile([P, width], U8, name="w1_plane_%d%d%d" % (a, g, t0), align_bytes=64)
+            nc.vector.quantize_mx(codes[:].bitcast(FP8X4), plane[:], rounded[a, g, t0][:])
+            first = t0 * (c1 - c0) // PASS
+            for u in range(width // P):
+                w1_codes[a, g, first + u] = codes[:, u * P : (u + 1) * P]
+                w1_planes[a, g, first + u] = plane[:, u * P : (u + 1) * P]
+
+        whole = [gather_words(a, 0, S) for a in range(K_PASSES - 1)]
+        v_codes = {(a, half): whole[a][:, half * BANK : (half + 1) * BANK] for a in range(2) for half in range(2)}
         v_planes = held.tile([P, S], U8, name="v_planes", align_bytes=64)
         nc.vector.tensor_copy(v_planes[:], tab_planes[:].indirect(offs_sb[:]))
-        v_codes.append(gather_words(1))
-        rounded0 = held.tile([P, PACK * PASS], BF16, name="rounded0", align_bytes=64)
-        round_w1(nc.scalar.copy, rounded0, raw00)
-        quantise_w1(0, 0, rounded0, 0, PACK, WORDS_AT[1])
-        v_codes.append(gather_words(2))
-        rounded1 = held.tile([P, PACK * PASS], BF16, name="rounded1", align_bytes=64)
-        round_w1(nc.scalar.copy, rounded1, raw10)
-        rounded2 = placed([P, PACK * PASS], BF16, "rounded2", WORDS_AT[2])
-        round_w1(nc.vector.tensor_copy, rounded2, raw20, 0, VECTOR_SHARE)
-        round_w1(nc.scalar.copy, rounded2, raw20, VECTOR_SHARE, P)
-        quantise_w1(1, 0, rounded1, 0, 1, LAST_RAW_AT)
-        quantise_w1(2, 0, rounded2, 0, 1)
-        quantise_w1(1, 0, rounded1, 1, 2, LAST_RAW_AT + KIB)
-        quantise_w1(2, 0, rounded2, 1, 2)
-        quantise_w1(1, 0, rounded1, 2, PACK, LAST_RAW_AT + 2 * KIB)
-        quantise_w1(2, 0, rounded2, 2, PACK)
-        for a in range(K_PASSES - 1):
-            rounded = placed([P, PACK * PASS], BF16, "rounded_late%d" % a, WORDS_AT[2])
-            round_w1(nc.vector.tensor_copy, rounded, raw_late[a])
-            quantise_w1(a, 1, rounded, 0, PACK)
+        for a in range(K_PASSES):
+            round_w1(nc.scalar.copy, a, 0)
+            quantise_w1(a, 0)
+        for half in range(2):
+            v_codes[2, half] = gather_words(2, half * BANK, (half + 1) * BANK)[:]
+        round_w1(nc.scalar.copy, 0, 1)
+        round_w1(nc.vector.tensor_copy, 1, 1)
+        quantise_w1(0, 1)
+        round_w1(nc.vector.tensor_copy, 2, 1)
+        quantise_w1(1, 1)
+        quantise_w1(2, 1)
 
-        def first_product(b, t):
+        def first_product(s):
+            g, u = SLICES[s]
             banks = [psum.tile([P, BANK], F32, name="bank") for half in range(2)]
             for half in range(2):
                 for a in range(K_PASSES):
-                    cols = slice(half * BANK, (half + 1) * BANK)
                     nc.tensor.matmul_mx(
                         banks[half][:],
-                        lhsT=w1_codes[a, b, t].bitcast(FP8X4),
-                        lhsT_scale=w1_planes[a, b][:, t * P : (t + 1) * P],
-                        rhs=v_codes[a][:, cols].bitcast(FP8X4),
-                        rhs_scale=v_planes[4 * a : P, cols],
+                        lhsT=w1_codes[a, g, u].bitcast(FP8X4),
+                        lhsT_scale=w1_planes[a, g, u],
+                        rhs=v_codes[a, half].bitcast(FP8X4),
+                        rhs_scale=v_planes[4 * a : P, half * BANK : (half + 1) * BANK],
                         start=(a == 0),
                         stop=(a == K_PASSES - 1),
                     )
             return banks
 
-        def cosine(banks, b, t):
-            folded = placed([P, S], F32, "folded_%d%d" % (b, t), FOLDED_AT[b][t])
-            h = ring.tile([P, S], F32, name="h", bufs=4)
+        def cosine(banks, s):
+            h = held.tile([P, S], F32, name="h_%d" % s)
+            folded = []
+            for half in range(2):
+                folded.append(placed([P, BANK], F32, "folded_%d%d" % (s, half), FOLDED_AT[s] + half * 2 * KIB))
+                nc.scalar.activation(folded[half][:], banks[half][:], ACT.Abs, bias=phase_column(s))
             for half in range(2):
                 cols = slice(half * BANK, (half + 1) * BANK)
-                nc.scalar.activation(folded[:, cols], banks[half][:], ACT.Abs, bias=phase_cols[:, b, t : t + 1])
-            for half in range(2):
-                cols = slice(half * BANK, (half + 1) * BANK)
-                nc.scalar.activation(h[:, cols], folded[:, cols], ACT.Sin, bias=math.pi / 2, scale=-1.0)
+                nc.scalar.activation(h[:, cols], folded[half][:], ACT.Sin, bias=math.pi / 2, scale=-1.0)
             return h
 
-        def pair_products(h, b, t, products):
-            left = ring.tile([P, PAIRS], F32, name="left")
-            width = PAIRS // 2
-            for m0 in range(0, PAIRS, width):
-                picks = pos1_sb[:, m0 // 16 : (m0 + width) // 16]
-                nc.vector.tensor_tensor(
-                    left[:, m0 : m0 + width], h[:].indirect(picks), gain_rows[b][:, t, m0 : m0 + width], ALU.mult
-                )
-            for m0 in range(0, PAIRS, width):
-                picks = pos2_sb[:, m0 // 16 : (m0 + width) // 16]
-                nc.vector.tensor_tensor(
-                    products[:, t, m0 : m0 + width], h[:].indirect(picks), left[:, m0 : m0 + width], ALU.mult
-                )
+        last = len(SLICES) - 1
+
+        def pair_products(h, s, into, m0, m1, width):
+            left = {}
+            for m in range(m0, m1, width):
+                if s == last:
+                    at = (LEFT_LOW_AT if m < HALF else ROUNDED_Z_AT[0, 0]) + 4 * m
+                else:
+                    at = LEFT_LOW_AT + 4 * m
+                left[m] = placed([P, width], F32, "left_%d_%d" % (s, m), at)
+                picks = pos1_sb[:, m // 16 : (m + width) // 16]
+                nc.vector.tensor_tensor(left[m][:], h[:].indirect(picks), gain_rows[:, s, 0:width], ALU.mult)
+            for m in range(m0, m1, width):
+                picks = pos2_sb[:, m // 16 : (m + width) // 16]
+                nc.vector.tensor_tensor(into[:, m : m + width], h[:].indirect(picks), left[m][:], ALU.mult)
 
         z_codes = [held.tile([P, PAIRS], U32, name="z_codes_%d" % b, align_bytes=64) for b in range(H_PASSES)]
         z_planes = [held.tile([P, PAIRS], U8, name="z_plane_%d" % b, align_bytes=64) for b in range(H_PASSES)]
+        products = [held.tile([P, PACK, PAIRS], F32, name="products_%d" % b) for b in range(H_PASSES)]
+        spare = held.tile([P, 2, PAIRS], F32, name="spare")
+        rounded_z = {}
 
-        def round_z(copy, rounded_z, b, m0, m1):
+        def round_z(copy, b, m0, m1):
+            shape, name = [P, PACK * (m1 - m0)], "rounded_z_%d_%d" % (b, m0)
+            if (b, m0) in ROUNDED_Z_AT:
+                rounded_z[b, m0] = placed(shape, BF16, name, ROUNDED_Z_AT[b, m0])
+            else:
+                rounded_z[b, m0] = held.tile(shape, BF16, name=name, align_bytes=64)
+            order = "p (e u) (c i) -> p c u e i" if b == 0 else "p (u e) (c i) -> p c u e i"
             copy(
-                rounded_z.rearrange("p (c i t) -> p c t i", i=4, t=PACK),
-                products[b][:, :, m0:m1].rearrange("p t (c i) -> p c t i", i=4),
+                rounded_z[b, m0][:].rearrange("p (c i u e) -> p c u e i", i=4, u=2, e=2),
+                products[b][:, :, m0:m1].rearrange(order, i=4, u=2),
             )
 
-        def quantise_z(rounded_z, b, m0, m1):
-            nc.vector.quantize_mx(z_codes[b][:, m0:m1].bitcast(FP8X4), z_planes[b][:, m0:m1], rounded_z)
+        def quantise_z(b, m0, m1):
+            nc.vector.quantize_mx(z_codes[b][:, m0:m1].bitcast(FP8X4), z_planes[b][:, m0:m1], rounded_z[b, m0][:])
 
-        products = [held.tile([P, PACK, PAIRS], F32, name="products_%d" % b) for b in range(H_PASSES)]
-        late_rounding = {1: (2, nc.scalar.copy)}
-        for b in range(H_PASSES):
-            for t in range(PACK):
-                h = cosine(first_product(b, t), b, t)
-                pair_products(h, b, t, products[b])
-                if b == 0 and t in late_rounding:
-                    a, copy = late_rounding[t]
-                    rounded = placed([P, PACK * PASS], BF16, "rounded_late%d" % a, LATE_AT[a])
-                    round_w1(copy, rounded, raw_late[a])
-                    quantise_w1(a, 1, rounded, 0, PACK)
-                if (b, t) == (0, PACK - 1):
-                    rounded = held.tile([P, PACK * PAIRS // 2], BF16, name="rounded_z0_low", align_bytes=64)
-                    round_z(nc.vector.tensor_copy, rounded[:], 0, 0, PAIRS // 2)
-                    quantise_z(rounded[:], 0, 0, PAIRS // 2)
-                if (b, t) == (1, PACK - 2):
-                    rounded = placed([P, PACK * PAIRS // 2], BF16, "rounded_z0_high", FOLDED_AT[b][t] + 2 * KIB)
-                    round_z(nc.scalar.copy, rounded[:], 0, PAIRS // 2, PAIRS)
-                    quantise_z(rounded[:], 0, PAIRS // 2, PAIRS)
+        targets = [products[0][:, 0, :], products[0][:, 1, :], spare[:, 0, :], spare[:, 1, :]]
+        targets = targets + [products[1][:, t, :] for t in range(PACK)]
+        for s in range(len(SLICES)):
+            h = cosine(first_product(s), s)
+            if s == 2:
+                round_w1(nc.scalar.copy, 1, 2, 2, 4)
+            if s == 3:
+                round_w1(nc.scalar.copy, 2, 2, 2, 4)
+            if s < last:
+                pair_products(h, s, targets[s], 0, PAIRS, HALF)
+            if s == 1:
+                nc.sync.dma_start(products[0][0:HALF_P, 2:4, :], products[0][HALF_P:P, 0:2, :])
+                round_w1(nc.scalar.copy, 0, 2)
+                round_w1(nc.vector.tensor_copy, 1, 2, 0, 2)
+                quantise_w1(0, 2)
+                round_w1(nc.vector.tensor_copy, 2, 2, 0, 2)
+                quantise_w1(1, 2, 0, 2)
+                quantise_w1(2, 2, 0, 2)
+            if s == 2:
+                quantise_w1(1, 2, 2, 4)
+            if s == 3:
+                quantise_w1(2, 2, 2, 4)
+                nc.sync.dma_start(products[0][HALF_P:P, 0:2, :], spare[0:HALF_P, :, :])
+                nc.sync.dma_start(products[0][HALF_P:P, 2:4, :], spare[HALF_P:P, :, :])
 
-        rounded_z1 = held.tile([P, PACK * PAIRS], BF16, name="rounded_z1", align_bytes=64)
-        round_z(nc.scalar.copy, rounded_z1[:, 0 : PACK * PAIRS // 2], 1, 0, PAIRS // 2)
-        round_z(nc.vector.tensor_copy, rounded_z1[:, PACK * PAIRS // 2 : PACK * PAIRS], 1, PAIRS // 2, PAIRS)
-        quantise_z(rounded_z1[:, 0 : PACK * PAIRS // 2], 1, 0, PAIRS // 2)
-        quantise_z(rounded_z1[:, PACK * PAIRS // 2 : PACK * PAIRS], 1, PAIRS // 2, PAIRS)
+        round_z(nc.scalar.copy, 0, 0, PAIRS)
+        pair_products(h, last, targets[last], 0, HALF, QUARTER)
+        quantise_z(0, 0, PAIRS)
+        round_z(nc.scalar.copy, 1, 0, HALF)
+        pair_products(h, last, targets[last], HALF, PAIRS, QUARTER)
+        round_z(nc.scalar.copy, 1, HALF, HALF + QUARTER)
+        quantise_z(1, 0, HALF)
+        round_z(nc.vector.tensor_copy, 1, HALF + QUARTER, PAIRS)
+        quantise_z(1, HALF, HALF + QUARTER)
+        quantise_z(1, HALF + QUARTER, PAIRS)
 
-        y_banks = [psum.tile([P, BANK], F32, name="bank") for i in range(N // P)]
-        for i in range(N // P):
-            for b in range(H_PASSES):
-                width = P if (i, b) == (0, H_PASSES - 1) else PAIRS
-                for m0 in range(0, PAIRS, width):
-                    nc.tensor.matmul_mx(
-                        y_banks[i][:, m0 : m0 + width],
-                        lhsT=w2_codes[:, b, 2 * i * P : 2 * (i + 1) * P].bitcast(FP4X4),
-                        lhsT_scale=w2_planes[:, b, i * P : (i + 1) * P],
-                        rhs=z_codes[b][:, m0 : m0 + width].bitcast(FP8X4),
-                        rhs_scale=z_planes[b][:, m0 : m0 + width],
-                        start=(b == 0),
-                        stop=(b == H_PASSES - 1 and m0 + width == PAIRS),
-                    )
         y_rows = [held.tile([P, PAIRS], F32, name="y_%d" % i) for i in range(N // P)]
         for i in range(N // P):
-            nc.scalar.copy(y_rows[i][:], y_banks[i][:])
+            for half in range(2):
+                bank = psum.tile([P, BANK], F32, name="bank")
+                for b in range(H_PASSES):
+                    for k in range(2):
+                        m0 = half * HALF + k * QUARTER
+                        nc.tensor.matmul_mx(
+                            bank[:, k * QUARTER : (k + 1) * QUARTER],
+                            lhsT=w2_codes[:, b, 2 * i * P : 2 * (i + 1) * P].bitcast(FP4X4),
+                            lhsT_scale=w2_planes[:, b, i * P : (i + 1) * P],
+                            rhs=z_codes[b][:, m0 : m0 + QUARTER].bitcast(FP8X4),
+                            rhs_scale=z_planes[b][:, m0 : m0 + QUARTER],
+                            start=(b == 0 and k == 0),
+                            stop=(b == H_PASSES - 1 and k == 1),
+                        )
+                nc.scalar.copy(y_rows[i][:, half * HALF : (half + 1) * HALF], bank[:, 0:HALF])
         for i in range(N // P):
             one_side = ring.tile([P, CONTRASTS], F32, name="one_side")
             diff = ring.tile([P, CONTRASTS], F32, name="diff")
-            width = CONTRASTS
-            for j0 in range(0, CONTRASTS, width):
-                picks = pos3_sb[:, j0 // 16 : (j0 + width) // 16]
-                nc.vector.tensor_copy(one_side[:, j0 : j0 + width], y_rows[i][:].indirect(picks))
-            for j0 in range(0, CONTRASTS, width):
-                picks = pos4_sb[:, j0 // 16 : (j0 + width) // 16]
-                nc.vector.tensor_tensor(
-                    diff[:, j0 : j0 + width], y_rows[i][:].indirect(picks), one_side[:, j0 : j0 + width], ALU.subtract
-                )
+            nc.vector.tensor_copy(one_side[:], y_rows[i][:].indirect(pos3_sb[:]))
+            nc.vector.tensor_tensor(diff[:], y_rows[i][:].indirect(pos4_sb[:]), one_side[:], ALU.subtract)
             squared = ring.tile([P, CONTRASTS], F32, name="squared", bufs=4)
             nc.scalar.activation(squared[:], diff[:], ACT.Square)
             queue = nc.scalar if i == N // P - 1 else nc.sync

@@ -285,28 +285,38 @@ def tile_list_echo_chamber_contrast_kernel(
         quantise_z(1, HALF + QUARTER, PAIRS)
 
         y_rows = [held.tile([P, PAIRS], F32, name="y_%d" % i) for i in range(N // P)]
-        for i in range(N // P):
-            for half in range(2):
-                bank = psum.tile([P, BANK], F32, name="bank")
-                for b in range(H_PASSES):
-                    for k in range(2):
-                        m0 = half * HALF + k * QUARTER
-                        nc.tensor.matmul_mx(
-                            bank[:, k * QUARTER : (k + 1) * QUARTER],
-                            lhsT=w2_codes[:, b, 2 * i * P : 2 * (i + 1) * P].bitcast(FP4X4),
-                            lhsT_scale=w2_planes[:, b, i * P : (i + 1) * P],
-                            rhs=z_codes[b][:, m0 : m0 + QUARTER].bitcast(FP8X4),
-                            rhs_scale=z_planes[b][:, m0 : m0 + QUARTER],
-                            start=(b == 0 and k == 0),
-                            stop=(b == H_PASSES - 1 and k == 1),
-                        )
-                nc.scalar.copy(y_rows[i][:, half * HALF : (half + 1) * HALF], bank[:, 0:HALF])
+
+        def second_product(i, c0, c1, width):
+            bank = psum.tile([P, BANK], F32, name="bank")
+            for b in range(H_PASSES):
+                for m0 in range(c0, c1, width):
+                    nc.tensor.matmul_mx(
+                        bank[:, m0 - c0 : m0 - c0 + width],
+                        lhsT=w2_codes[:, b, 2 * i * P : 2 * (i + 1) * P].bitcast(FP4X4),
+                        lhsT_scale=w2_planes[:, b, i * P : (i + 1) * P],
+                        rhs=z_codes[b][:, m0 : m0 + width].bitcast(FP8X4),
+                        rhs_scale=z_planes[b][:, m0 : m0 + width],
+                        start=(b == 0 and m0 == c0),
+                        stop=(b == H_PASSES - 1 and m0 + width == c1),
+                    )
+            nc.scalar.copy(y_rows[i][:, c0:c1], bank[:, 0 : c1 - c0])
+
+        second_product(0, 0, HALF, QUARTER)
+        second_product(0, HALF, HALF + QUARTER, QUARTER)
+        second_product(0, HALF + QUARTER, PAIRS, QUARTER)
+        second_product(1, 0, HALF, QUARTER)
+        second_product(1, HALF, PAIRS, QUARTER)
+        for i in range(2, N // P):
+            second_product(i, 0, PAIRS, PAIRS)
         for i in range(N // P):
             one_side = ring.tile([P, CONTRASTS], F32, name="one_side")
-            diff = ring.tile([P, CONTRASTS], F32, name="diff")
             nc.vector.tensor_copy(one_side[:], y_rows[i][:].indirect(pos3_sb[:]))
-            nc.vector.tensor_tensor(diff[:], y_rows[i][:].indirect(pos4_sb[:]), one_side[:], ALU.subtract)
-            squared = ring.tile([P, CONTRASTS], F32, name="squared", bufs=4)
-            nc.scalar.activation(squared[:], diff[:], ACT.Square)
-            queue = nc.scalar if i == N // P - 1 else nc.sync
-            queue.dma_start(out[i * P : (i + 1) * P, :], squared[:])
+            width = CONTRASTS // 2 if i == N // P - 1 else CONTRASTS
+            for j0 in range(0, CONTRASTS, width):
+                diff = ring.tile([P, width], F32, name="diff" if j0 == 0 else "diff_last", bufs=2)
+                picks = pos4_sb[:, j0 // 16 : (j0 + width) // 16]
+                nc.vector.tensor_tensor(diff[:], y_rows[i][:].indirect(picks), one_side[:, j0 : j0 + width], ALU.subtract)
+                squared = ring.tile([P, width], F32, name="squared", bufs=5)
+                nc.scalar.activation(squared[:], diff[:], ACT.Square)
+                queue = nc.scalar if (i, j0 + width) == (N // P - 1, CONTRASTS) else nc.sync
+                queue.dma_start(out[i * P : (i + 1) * P, j0 : j0 + width], squared[:])

@@ -24,24 +24,50 @@ PASS = P * PACK
 BANK = 512
 K_PASSES = K // PASS
 H_PASSES = H // PASS
-KIB = 1024
 HALF = PAIRS // 2
 QUARTER = PAIRS // 4
 COLUMN_GROUPS = [(0, 256), (256, 512), (512, 1024)]
 SLICES = [(0, 0), (0, 1), (1, 0), (1, 1), (2, 0), (2, 1), (2, 2), (2, 3)]
-EARLY_RAW_AT = 2 * KIB
-LATE_RAW_AT = [8 * KIB, 16 * KIB, 34 * KIB]
-LEFT_LOW_AT = 28 * KIB
-ROUNDED_AT = {
-    (2, 1, 0): LEFT_LOW_AT,
-    (0, 2, 0): EARLY_RAW_AT - 2 * KIB,
-    (1, 2, 0): LEFT_LOW_AT - KIB - KIB // 2,
-    (1, 2, 2): LATE_RAW_AT[0],
-    (2, 2, 0): LEFT_LOW_AT + KIB + KIB // 2,
-    (2, 2, 2): LATE_RAW_AT[1],
+GAIN_WIDTH = 512
+KIB = 1024
+RING_KINDS = ("folded", "left", "h")
+PLACES = {
+    "raw_20": 38 * KIB,
+    "v_codes_2_768": 38 * KIB,
+    "folded_0_768": 9 * KIB,
+    "w1_codes_210": 9 * KIB,
+    "raw_02": 12 * KIB,
+    "folded_2_0": 18 * KIB,
+    "folded_2_512": 12 * KIB,
+    "w1_codes_020": 17 * KIB,
+    "w1_codes_120": 19 * KIB,
+    "folded_3_0": 11 * KIB,
+    "rounded_222": 11 * KIB,
+    "raw_12": 24 * KIB,
+    "spare": 24 * KIB,
+    "raw_21": 32 * KIB,
+    "left_1_0": 32 * KIB,
+    "left_1_256": 33 * KIB,
+    "tab_planes": 36 * KIB,
+    "w1_codes_000": 36 * KIB,
+    "w1_codes_100": 37 * KIB,
+    "folded_6_0": 20 * KIB,
+    "rounded_z_0_0": 20 * KIB,
+    "folded_3_512": 13 * KIB,
+    "w1_codes_122": 13 * KIB,
+    "rounded_z_0_256": 22 * KIB,
+    "left_7_256": 22 * KIB,
+    "left_7_384": 23 * KIB,
+    "tab_words_0": 48 * KIB,
+    "products_1": 48 * KIB,
+    "tab_words_1": 56 * KIB,
+    "y_0": 56 * KIB,
+    "y_1": 58 * KIB,
+    "y_2": 60 * KIB,
+    "y_3": 62 * KIB,
 }
-FOLDED_AT = [EARLY_RAW_AT] * 2 + [LATE_RAW_AT[0]] + [LATE_RAW_AT[1]] + [LATE_RAW_AT[2]] * 4
-ROUNDED_Z_AT = {(0, 0): LATE_RAW_AT[2] - 2 * KIB}
+FIRST_BANKS = [0, 1, 2, 3, 1, 4, 5, 6, 7, 0, 2, 3, 1, 4, 5, 6, 7]
+SECOND_BANKS = [0, 2, 3, 1, 4, 5, 6]
 
 
 def tile_list_echo_chamber_contrast_kernel(
@@ -52,10 +78,15 @@ def tile_list_echo_chamber_contrast_kernel(
         held = ctx.enter_context(tc.tile_pool(name="held", bufs=1))
         reused = ctx.enter_context(tc.tile_pool(name="reused", bufs=1))
         ring = ctx.enter_context(tc.tile_pool(name="ring", bufs=3))
-        psum = ctx.enter_context(tc.psum_pool(name="psum", bufs=8))
+        psum = ctx.enter_context(tc.psum_pool(name="psum", bufs=1))
 
-        def placed(shape, dtype, name, at):
-            return reused.tile(shape, dtype, name=name, align_bytes=64, offset=at)
+        def tile(shape, dtype, name):
+            if name in PLACES:
+                return reused.tile(shape, dtype, name=name, align_bytes=64, offset=PLACES[name])
+            kind = name.split("_")[0]
+            if kind in RING_KINDS:
+                return ring.tile(shape, dtype, name=name, tag=kind, bufs=4, align_bytes=64)
+            return held.tile(shape, dtype, name=name, align_bytes=64)
 
         def load_list(name, src):
             t = held.tile(list(src.shape), U16, name=name)
@@ -63,14 +94,13 @@ def tile_list_echo_chamber_contrast_kernel(
             return t
 
         def load_table_words(a):
-            t = held.tile([P, T], I32, name="tab_words_%d" % a)
+            t = tile([P, T], I32, "tab_words_%d" % a)
             nc.sync.dma_start(t[:], tab_words[a].rearrange("p t i -> p (t i)").bitcast(I32))
             return t
 
-        def load_w1(a, g, at=None):
+        def load_w1(a, g):
             c0, c1 = COLUMN_GROUPS[g]
-            shape, name = [P, PACK, c1 - c0], "w1_raw_%d_%d" % (a, g)
-            t = held.tile(shape, F32, name=name) if at is None else placed(shape, F32, name, at)
+            t = tile([P, PACK, c1 - c0], F32, "raw_%d%d" % (a, g))
             rows = w1[a * PASS : (a + 1) * PASS, c0:c1]
             nc.sync.dma_start(t[:], rows.rearrange("(p j) c -> p j c", j=PACK))
             return t
@@ -87,7 +117,7 @@ def tile_list_echo_chamber_contrast_kernel(
             queue.dma_start(t[:], vec[PASS : 2 * PASS].rearrange("(p t) -> p t", t=PACK))
             return t
 
-        tab_planes = held.tile([P, T], U8, name="tab_planes")
+        tab_planes = tile([P, T], U8, "tab_planes")
         nc.vector.memset(tab_planes[:].bitcast(I32), 0)
         gain_folded = load_folded_columns("gain_folded", gain)
         gain_plain = load_plain_columns(nc.scalar, "gain_plain", gain)
@@ -105,21 +135,20 @@ def tile_list_echo_chamber_contrast_kernel(
                 tab_scales[:, 4 * q : 4 * q + 4, :].bitcast(I32),
             )
         raw[1, 0] = load_w1(1, 0)
-        raw[2, 0] = load_w1(2, 0)
         words.append(load_table_words(2))
-        raw[0, 1] = load_w1(0, 1, EARLY_RAW_AT)
-        raw[1, 1] = load_w1(1, 1)
-        raw[2, 1] = load_w1(2, 1)
+        raw[2, 0] = load_w1(2, 0)
+        for a in range(K_PASSES):
+            raw[a, 1] = load_w1(a, 1)
         pos1_sb = load_list("pos1_sb", pos1)
         pos2_sb = load_list("pos2_sb", pos2)
         phase_plain = load_plain_columns(nc.sync, "phase_plain", phase)
         for a in range(K_PASSES):
-            raw[a, 2] = load_w1(a, 2, LATE_RAW_AT[a])
-        w2_codes = held.tile([P, H_PASSES, 2 * N], U8, name="w2_codes", align_bytes=64)
+            raw[a, 2] = load_w1(a, 2)
+        w2_codes = tile([P, H_PASSES, 2 * N], U8, "w2_codes")
         nc.sync.dma_start(w2_codes[:].bitcast(I32), w2_words.rearrange("b p c -> p b c").bitcast(I32))
         pos3_sb = load_list("pos3_sb", pos3)
         pos4_sb = load_list("pos4_sb", pos4)
-        w2_planes = held.tile([P, H_PASSES, N], U8, name="w2_planes", align_bytes=64)
+        w2_planes = tile([P, H_PASSES, N], U8, "w2_planes")
         nc.vector.memset(w2_planes[:].bitcast(I32), 0)
         for q in range(4):
             nc.sync.dma_start(
@@ -127,187 +156,227 @@ def tile_list_echo_chamber_contrast_kernel(
                 w2_scales[:, 4 * q : 4 * q + 4, :].rearrange("b r c -> r b c").bitcast(I32),
             )
 
-        gain_rows = held.tile([P, len(SLICES), HALF], F32, name="gain_rows")
-        nc.scalar.copy(
-            gain_rows[:, 0:4, :].rearrange("p (g u) m -> p g u m", g=2),
-            gain_folded[:, :, 0:3:2].unsqueeze(3).to_broadcast([P, 2, 2, HALF]),
-        )
-        nc.scalar.copy(gain_rows[:, 4:8, :], gain_plain[:].unsqueeze(2).to_broadcast([P, PACK, HALF]))
+        gain_rows = [tile([P, GAIN_WIDTH], F32, "gain_row_%d" % s) for s in range(len(SLICES))]
+        for s in range(len(SLICES)):
+            g, u = SLICES[s]
+            column = gain_folded[:, g, 2 * u : 2 * u + 1] if g < 2 else gain_plain[:, u : u + 1]
+            nc.scalar.copy(gain_rows[s][:], column.to_broadcast([P, GAIN_WIDTH]))
 
         def phase_column(s):
             g, u = SLICES[s]
             return phase_folded[:, g, 2 * u : 2 * u + 1] if g < 2 else phase_plain[:, u : u + 1]
 
+        v_codes = {}
+        v_planes = tile([P, S], U8, "v_planes")
+
         def gather_words(a, j0, j1):
-            t = held.tile([P, j1 - j0], U32, name="v_codes_%d_%d" % (a, j0), align_bytes=64)
-            nc.vector.tensor_copy(t[:], words[a][:].bitcast(U32).indirect(offs_sb[:, j0 // 16 : j1 // 16]))
-            return t
+            v_codes[a, j0, j1] = tile([P, j1 - j0], U32, "v_codes_%d_%d" % (a, j0))
+            picks = offs_sb[:, j0 // 16 : j1 // 16]
+            nc.vector.tensor_copy(v_codes[a, j0, j1][:], words[a][:].bitcast(U32).indirect(picks))
 
         rounded, w1_codes, w1_planes = {}, {}, {}
 
         def round_w1(copy, a, g, t0=0, t1=PACK):
             c0, c1 = COLUMN_GROUPS[g]
-            shape, name = [P, (t1 - t0) * (c1 - c0)], "rounded_%d%d%d" % (a, g, t0)
-            if (a, g, t0) in ROUNDED_AT:
-                rounded[a, g, t0] = placed(shape, BF16, name, ROUNDED_AT[a, g, t0])
-            else:
-                rounded[a, g, t0] = held.tile(shape, BF16, name=name, align_bytes=64)
+            rounded[a, g, t0] = tile([P, (t1 - t0) * (c1 - c0)], BF16, "rounded_%d%d%d" % (a, g, t0))
             copy(
-                rounded[a, g, t0][:].rearrange("p (t m j) -> p m j t", t=t1 - t0, j=PACK),
-                raw[a, g][:].rearrange("p j (m t) -> p m j t", t=PACK)[:, :, :, t0:t1],
+                rounded[a, g, t0][:].rearrange("p (u e m j) -> p u m j e", u=(t1 - t0) // 2, e=2, j=PACK),
+                raw[a, g][:].rearrange("p j (m u e) -> p u m j e", u=2, e=2)[:, t0 // 2 : t1 // 2],
             )
 
         def quantise_w1(a, g, t0=0, t1=PACK):
             c0, c1 = COLUMN_GROUPS[g]
             width = (t1 - t0) * (c1 - c0) // PACK
-            codes = held.tile([P, width], U32, name="w1_codes_%d%d%d" % (a, g, t0), align_bytes=64)
-            plane = held.tile([P, width], U8, name="w1_plane_%d%d%d" % (a, g, t0), align_bytes=64)
+            codes = tile([P, width], U32, "w1_codes_%d%d%d" % (a, g, t0))
+            plane = tile([P, width], U8, "w1_plane_%d%d%d" % (a, g, t0))
             nc.vector.quantize_mx(codes[:].bitcast(FP8X4), plane[:], rounded[a, g, t0][:])
             first = t0 * (c1 - c0) // PASS
             for u in range(width // P):
                 w1_codes[a, g, first + u] = codes[:, u * P : (u + 1) * P]
                 w1_planes[a, g, first + u] = plane[:, u * P : (u + 1) * P]
 
-        whole = [gather_words(a, 0, S) for a in range(K_PASSES - 1)]
-        v_codes = {(a, half): whole[a][:, half * BANK : (half + 1) * BANK] for a in range(2) for half in range(2)}
-        v_planes = held.tile([P, S], U8, name="v_planes", align_bytes=64)
-        nc.vector.tensor_copy(v_planes[:], tab_planes[:].indirect(offs_sb[:]))
-        for a in range(K_PASSES):
-            round_w1(nc.scalar.copy, a, 0)
-            quantise_w1(a, 0)
-        for half in range(2):
-            v_codes[2, half] = gather_words(2, half * BANK, (half + 1) * BANK)[:]
-        round_w1(nc.scalar.copy, 0, 1)
-        round_w1(nc.vector.tensor_copy, 1, 1)
-        quantise_w1(0, 1)
-        round_w1(nc.vector.tensor_copy, 2, 1)
-        quantise_w1(1, 1)
-        quantise_w1(2, 1)
+        def bank(number, name):
+            return psum.tile([P, BANK], F32, name=name, offset=number * 4 * BANK)
 
-        def first_product(s):
+        banks, folded, h_rows, lefts = {}, {}, {}, {}
+
+        def first_product(s, j0, j1, passes=range(K_PASSES)):
             g, u = SLICES[s]
-            banks = [psum.tile([P, BANK], F32, name="bank") for half in range(2)]
-            for half in range(2):
-                for a in range(K_PASSES):
-                    nc.tensor.matmul_mx(
-                        banks[half][:],
-                        lhsT=w1_codes[a, g, u].bitcast(FP8X4),
-                        lhsT_scale=w1_planes[a, g, u],
-                        rhs=v_codes[a, half].bitcast(FP8X4),
-                        rhs_scale=v_planes[4 * a : P, half * BANK : (half + 1) * BANK],
-                        start=(a == 0),
-                        stop=(a == K_PASSES - 1),
-                    )
-            return banks
+            if (s, j0) not in banks:
+                banks[s, j0] = bank(FIRST_BANKS[len(banks)], "bank_%d_%d" % (s, j0))
+            for a in passes:
+                for (held_a, c0, c1), codes in v_codes.items():
+                    lo, hi = max(j0, c0), min(j1, c1)
+                    if held_a == a and lo < hi:
+                        nc.tensor.matmul_mx(
+                            banks[s, j0][:, lo - j0 : hi - j0],
+                            lhsT=w1_codes[a, g, u].bitcast(FP8X4),
+                            lhsT_scale=w1_planes[a, g, u],
+                            rhs=codes[:, lo - c0 : hi - c0].bitcast(FP8X4),
+                            rhs_scale=v_planes[4 * a : P, lo:hi],
+                            start=(a == 0),
+                            stop=(a == K_PASSES - 1 and hi == j1),
+                        )
 
-        def cosine(banks, s):
-            h = held.tile([P, S], F32, name="h_%d" % s)
-            folded = []
-            for half in range(2):
-                folded.append(placed([P, BANK], F32, "folded_%d%d" % (s, half), FOLDED_AT[s] + half * 2 * KIB))
-                nc.scalar.activation(folded[half][:], banks[half][:], ACT.Abs, bias=phase_column(s))
-            for half in range(2):
-                cols = slice(half * BANK, (half + 1) * BANK)
-                nc.scalar.activation(h[:, cols], folded[half][:], ACT.Sin, bias=math.pi / 2, scale=-1.0)
-            return h
+        def fold(s, j0, j1):
+            folded[s, j0] = tile([P, j1 - j0], F32, "folded_%d_%d" % (s, j0))
+            nc.scalar.activation(folded[s, j0][:], banks[s, j0][:, 0 : j1 - j0], ACT.Abs, bias=phase_column(s))
 
-        last = len(SLICES) - 1
+        def sine(s, j0, j1):
+            if s not in h_rows:
+                h_rows[s] = tile([P, S], F32, "h_%d" % s)
+            nc.scalar.activation(h_rows[s][:, j0:j1], folded[s, j0][:], ACT.Sin, bias=math.pi / 2, scale=-1.0)
 
-        def pair_products(h, s, into, m0, m1, width):
-            left = {}
-            for m in range(m0, m1, width):
-                if s == last:
-                    at = (LEFT_LOW_AT if m < HALF else ROUNDED_Z_AT[0, 0]) + 4 * m
-                else:
-                    at = LEFT_LOW_AT + 4 * m
-                left[m] = placed([P, width], F32, "left_%d_%d" % (s, m), at)
-                picks = pos1_sb[:, m // 16 : (m + width) // 16]
-                nc.vector.tensor_tensor(left[m][:], h[:].indirect(picks), gain_rows[:, s, 0:width], ALU.mult)
-            for m in range(m0, m1, width):
-                picks = pos2_sb[:, m // 16 : (m + width) // 16]
-                nc.vector.tensor_tensor(into[:, m : m + width], h[:].indirect(picks), left[m][:], ALU.mult)
+        def cosine(s):
+            for j0 in (0, BANK):
+                first_product(s, j0, j0 + BANK)
+            for j0 in (0, BANK):
+                fold(s, j0, j0 + BANK)
+            for j0 in (0, BANK):
+                sine(s, j0, j0 + BANK)
 
-        z_codes = [held.tile([P, PAIRS], U32, name="z_codes_%d" % b, align_bytes=64) for b in range(H_PASSES)]
-        z_planes = [held.tile([P, PAIRS], U8, name="z_plane_%d" % b, align_bytes=64) for b in range(H_PASSES)]
-        products = [held.tile([P, PACK, PAIRS], F32, name="products_%d" % b) for b in range(H_PASSES)]
-        spare = held.tile([P, 2, PAIRS], F32, name="spare")
+        z_codes = [tile([P, PAIRS], U32, "z_codes_%d" % b) for b in range(H_PASSES)]
+        z_planes = [tile([P, PAIRS], U8, "z_plane_%d" % b) for b in range(H_PASSES)]
+        products = [tile([P, PACK, PAIRS], F32, "products_%d" % b) for b in range(H_PASSES)]
+        spare = tile([P, 2, PAIRS], F32, "spare")
+        targets = [products[0][:, 0, :], products[0][:, 1, :], spare[:, 0, :], spare[:, 1, :]]
+        targets = targets + [products[1][:, t, :] for t in range(PACK)]
+
+        def first_factor(s, m0=0, m1=PAIRS):
+            lefts[s, m0] = tile([P, m1 - m0], F32, "left_%d_%d" % (s, m0))
+            picks = pos1_sb[:, m0 // 16 : m1 // 16]
+            nc.vector.tensor_tensor(lefts[s, m0][:], h_rows[s][:].indirect(picks), gain_rows[s][:, 0 : m1 - m0], ALU.mult)
+
+        def pair_product(s, m0=0, m1=PAIRS):
+            picks = pos2_sb[:, m0 // 16 : m1 // 16]
+            nc.vector.tensor_tensor(targets[s][:, m0:m1], h_rows[s][:].indirect(picks), lefts[s, m0][:], ALU.mult)
+
+        def pairs_in_halves(s, m0=0, m1=PAIRS):
+            mid = (m0 + m1) // 2
+            first_factor(s, m0, mid)
+            first_factor(s, mid, m1)
+            pair_product(s, m0, mid)
+            pair_product(s, mid, m1)
+
         rounded_z = {}
 
         def round_z(copy, b, m0, m1):
-            shape, name = [P, PACK * (m1 - m0)], "rounded_z_%d_%d" % (b, m0)
-            if (b, m0) in ROUNDED_Z_AT:
-                rounded_z[b, m0] = placed(shape, BF16, name, ROUNDED_Z_AT[b, m0])
-            else:
-                rounded_z[b, m0] = held.tile(shape, BF16, name=name, align_bytes=64)
+            rounded_z[b, m0] = tile([P, PACK * (m1 - m0)], BF16, "rounded_z_%d_%d" % (b, m0))
             order = "p (e u) (c i) -> p c u e i" if b == 0 else "p (u e) (c i) -> p c u e i"
             copy(
-                rounded_z[b, m0][:].rearrange("p (c i u e) -> p c u e i", i=4, u=2, e=2),
-                products[b][:, :, m0:m1].rearrange(order, i=4, u=2),
+                rounded_z[b, m0][:].rearrange("p (c i u e) -> p c u e i", i=2, u=2, e=2),
+                products[b][:, :, m0:m1].rearrange(order, i=2, u=2),
             )
 
         def quantise_z(b, m0, m1):
             nc.vector.quantize_mx(z_codes[b][:, m0:m1].bitcast(FP8X4), z_planes[b][:, m0:m1], rounded_z[b, m0][:])
 
-        targets = [products[0][:, 0, :], products[0][:, 1, :], spare[:, 0, :], spare[:, 1, :]]
-        targets = targets + [products[1][:, t, :] for t in range(PACK)]
-        for s in range(len(SLICES)):
-            h = cosine(first_product(s), s)
-            if s == 2:
-                round_w1(nc.scalar.copy, 1, 2, 2, 4)
-            if s == 3:
-                round_w1(nc.scalar.copy, 2, 2, 2, 4)
-            if s < last:
-                pair_products(h, s, targets[s], 0, PAIRS, HALF)
-            if s == 1:
-                nc.sync.dma_start(products[0][0:HALF_P, 2:4, :], products[0][HALF_P:P, 0:2, :])
-                round_w1(nc.scalar.copy, 0, 2)
-                round_w1(nc.vector.tensor_copy, 1, 2, 0, 2)
-                quantise_w1(0, 2)
-                round_w1(nc.vector.tensor_copy, 2, 2, 0, 2)
-                quantise_w1(1, 2, 0, 2)
-                quantise_w1(2, 2, 0, 2)
-            if s == 2:
-                quantise_w1(1, 2, 2, 4)
-            if s == 3:
-                quantise_w1(2, 2, 2, 4)
-                nc.sync.dma_start(products[0][HALF_P:P, 0:2, :], spare[0:HALF_P, :, :])
-                nc.sync.dma_start(products[0][HALF_P:P, 2:4, :], spare[HALF_P:P, :, :])
+        y_rows = [tile([P, PAIRS], F32, "y_%d" % i) for i in range(N // P)]
+        y_banks = {}
 
-        round_z(nc.scalar.copy, 0, 0, PAIRS)
-        pair_products(h, last, targets[last], 0, HALF, QUARTER)
-        quantise_z(0, 0, PAIRS)
-        round_z(nc.scalar.copy, 1, 0, HALF)
-        pair_products(h, last, targets[last], HALF, PAIRS, QUARTER)
-        round_z(nc.scalar.copy, 1, HALF, HALF + QUARTER)
+        def second_product(i, c0, c1, b, m0, m1, start, stop):
+            if (i, c0) not in y_banks:
+                y_banks[i, c0] = bank(SECOND_BANKS[len(y_banks)], "y_bank_%d_%d" % (i, c0))
+            nc.tensor.matmul_mx(
+                y_banks[i, c0][:, m0 - c0 : m1 - c0],
+                lhsT=w2_codes[:, b, 2 * i * P : 2 * (i + 1) * P].bitcast(FP4X4),
+                lhsT_scale=w2_planes[:, b, i * P : (i + 1) * P],
+                rhs=z_codes[b][:, m0:m1].bitcast(FP8X4),
+                rhs_scale=z_planes[b][:, m0:m1],
+                start=start,
+                stop=stop,
+            )
+
+        def copy_y(i, c0, c1):
+            nc.scalar.copy(y_rows[i][:, c0:c1], y_banks[i, c0][:, 0 : c1 - c0])
+
+
+        on_scalar, on_vector = nc.scalar.copy, nc.vector.tensor_copy
+        gather_words(0, 0, S)
+        gather_words(1, 0, S)
+        nc.vector.tensor_copy(v_planes[:], tab_planes[:].indirect(offs_sb[:]))
+        for a in range(K_PASSES - 1):
+            round_w1(on_scalar, a, 0)
+            quantise_w1(a, 0)
+        gather_words(2, 0, 512)
+        gather_words(2, 512, 768)
+        round_w1(on_scalar, 2, 0, 0, 2)
+        round_w1(on_scalar, 2, 0, 2, 4)
+        quantise_w1(2, 0, 0, 2)
+        gather_words(2, 768, S)
+        quantise_w1(2, 0, 2, 4)
+        for j0, j1 in ((0, 512), (512, 768), (768, S)):
+            first_product(0, j0, j1, range(2))
+        for j0, j1 in ((0, 512), (512, 768), (768, S)):
+            first_product(0, j0, j1, range(2, 3))
+        fold(0, 0, 512)
+        fold(0, 512, 768)
+        sine(0, 0, 512)
+        fold(0, 768, S)
+        sine(0, 512, 768)
+        sine(0, 768, S)
+        for a in range(K_PASSES - 1):
+            round_w1(on_vector, a, 1)
+            quantise_w1(a, 1)
+        round_w1(on_vector, 2, 1)
+        cosine(1)
+        first_factor(0)
+        quantise_w1(2, 1)
+        pair_product(0)
+        round_w1(on_scalar, 0, 2)
+        pairs_in_halves(1)
+        nc.sync.dma_start(products[0][0:HALF_P, 2:4, :], products[0][HALF_P:P, 0:2, :])
+        round_w1(on_vector, 1, 2, 0, 2)
+        cosine(2)
+        quantise_w1(0, 2)
+        quantise_w1(1, 2, 0, 2)
+        round_w1(on_scalar, 1, 2, 2, 4)
+        first_factor(2)
+        round_w1(on_vector, 2, 2, 0, 2)
+        pair_product(2)
+        quantise_w1(2, 2, 0, 2)
+        cosine(3)
+        round_w1(on_scalar, 2, 2, 2, 4)
+        first_factor(3)
+        quantise_w1(1, 2, 2, 4)
+        pair_product(3)
+        nc.sync.dma_start(products[0][HALF_P:P, 0:2, :], spare[0:HALF_P, :, :])
+        nc.sync.dma_start(products[0][HALF_P:P, 2:4, :], spare[HALF_P:P, :, :])
+        quantise_w1(2, 2, 2, 4)
+        for s in (4, 5, 6):
+            cosine(s)
+            pairs_in_halves(s)
+        round_z(on_scalar, 0, 0, HALF)
+        quantise_z(0, 0, HALF)
+        cosine(7)
+
+        last = len(SLICES) - 1
+        q3 = HALF + QUARTER
+        round_z(on_scalar, 0, HALF, PAIRS)
+        pairs_in_halves(last, 0, HALF)
+        quantise_z(0, HALF, PAIRS)
+        round_z(on_scalar, 1, 0, HALF)
+        pairs_in_halves(last, HALF, PAIRS)
+        round_z(on_scalar, 1, HALF, q3)
         quantise_z(1, 0, HALF)
-        round_z(nc.vector.tensor_copy, 1, HALF + QUARTER, PAIRS)
-        quantise_z(1, HALF, HALF + QUARTER)
-        quantise_z(1, HALF + QUARTER, PAIRS)
+        round_z(on_vector, 1, q3, PAIRS)
+        quantise_z(1, HALF, q3)
+        quantise_z(1, q3, PAIRS)
 
-        y_rows = [held.tile([P, PAIRS], F32, name="y_%d" % i) for i in range(N // P)]
-
-        def second_product(i, c0, c1, width):
-            bank = psum.tile([P, BANK], F32, name="bank")
+        def y_piece(i, c0, c1, widths):
             for b in range(H_PASSES):
-                for m0 in range(c0, c1, width):
-                    nc.tensor.matmul_mx(
-                        bank[:, m0 - c0 : m0 - c0 + width],
-                        lhsT=w2_codes[:, b, 2 * i * P : 2 * (i + 1) * P].bitcast(FP4X4),
-                        lhsT_scale=w2_planes[:, b, i * P : (i + 1) * P],
-                        rhs=z_codes[b][:, m0 : m0 + width].bitcast(FP8X4),
-                        rhs_scale=z_planes[b][:, m0 : m0 + width],
-                        start=(b == 0 and m0 == c0),
-                        stop=(b == H_PASSES - 1 and m0 + width == c1),
-                    )
-            nc.scalar.copy(y_rows[i][:, c0:c1], bank[:, 0 : c1 - c0])
+                for m0 in range(c0, c1, widths[b]):
+                    m1 = m0 + widths[b]
+                    second_product(i, c0, c1, b, m0, m1, b == 0 and m0 == c0, b == H_PASSES - 1 and m1 == c1)
+            copy_y(i, c0, c1)
 
-        second_product(0, 0, HALF, QUARTER)
-        second_product(0, HALF, HALF + QUARTER, QUARTER)
-        second_product(0, HALF + QUARTER, PAIRS, QUARTER)
-        second_product(1, 0, HALF, QUARTER)
-        second_product(1, HALF, PAIRS, QUARTER)
+        y_piece(0, 0, HALF, (HALF, HALF))
+        y_piece(0, HALF, q3, (QUARTER, QUARTER))
+        y_piece(0, q3, PAIRS, (QUARTER, QUARTER))
+        y_piece(1, 0, HALF, (HALF, HALF))
+        y_piece(1, HALF, PAIRS, (HALF, HALF))
         for i in range(2, N // P):
-            second_product(i, 0, PAIRS, PAIRS)
+            y_piece(i, 0, PAIRS, (HALF, PAIRS))
         for i in range(N // P):
             one_side = ring.tile([P, CONTRASTS], F32, name="one_side")
             nc.vector.tensor_copy(one_side[:], y_rows[i][:].indirect(pos3_sb[:]))

@@ -264,8 +264,8 @@ def tile_list_echo_chamber_contrast_kernel(
             rounded_z[b, m0] = tile([P, PACK * (m1 - m0)], BF16, "rounded_z_%d_%d" % (b, m0))
             order = "p (e u) (c i) -> p c u e i" if b == 0 else "p (u e) (c i) -> p c u e i"
             copy(
-                rounded_z[b, m0][:].rearrange("p (c i u e) -> p c u e i", i=2, u=2, e=2),
-                products[b][:, :, m0:m1].rearrange(order, i=2, u=2),
+                rounded_z[b, m0][:].rearrange("p (c i u e) -> p c u e i", i=4, u=2, e=2),
+                products[b][:, :, m0:m1].rearrange(order, i=4, u=2),
             )
 
         def quantise_z(b, m0, m1):

@@ -16,58 +16,27 @@ FP8X4 = mybir.dt.float8_e4m3fn_x4
 FP4X4 = mybir.dt.float4_e2m1fn_x4
 ACT = mybir.ActivationFunctionType
 ALU = mybir.AluOpType
+BYTES_OF = {F32: 4, I32: 4, U32: 4, BF16: 2, U8: 1}
 
 P = 128
 HALF_P = P // 2
+QUADRANT = 32
 PACK = 4
 PASS = P * PACK
 BANK = 512
+BANKS = 8
+LIST_ROWS = 16
 K_PASSES = K // PASS
 H_PASSES = H // PASS
 HALF = PAIRS // 2
 QUARTER = PAIRS // 4
 COLUMN_GROUPS = [(0, 256), (256, 512), (512, 1024)]
-SLICES = [(0, 0), (0, 1), (1, 0), (1, 1), (2, 0), (2, 1), (2, 2), (2, 3)]
-GAIN_WIDTH = 512
+SLICES = [(g, u) for g in range(2) for u in range(2)] + [(2, t) for t in range(PACK)]
+LOW_T, HIGH_T, ALL_T = (0, 2), (2, 4), (0, 4)
+EARLY_GAIN_ROWS = 5
+RING = 4
 KIB = 1024
-RING_KINDS = ("folded", "left", "h")
-PLACES = {
-    "raw_20": 38 * KIB,
-    "v_codes_2_768": 38 * KIB,
-    "folded_0_768": 9 * KIB,
-    "w1_codes_210": 9 * KIB,
-    "raw_02": 12 * KIB,
-    "folded_2_0": 18 * KIB,
-    "folded_2_512": 12 * KIB,
-    "w1_codes_020": 17 * KIB,
-    "w1_codes_120": 19 * KIB,
-    "folded_3_0": 11 * KIB,
-    "rounded_222": 11 * KIB,
-    "raw_12": 24 * KIB,
-    "spare": 24 * KIB,
-    "raw_21": 32 * KIB,
-    "left_1_0": 32 * KIB,
-    "left_1_256": 33 * KIB,
-    "tab_planes": 36 * KIB,
-    "w1_codes_000": 36 * KIB,
-    "w1_codes_100": 37 * KIB,
-    "folded_6_0": 20 * KIB,
-    "rounded_z_0_0": 20 * KIB,
-    "folded_3_512": 13 * KIB,
-    "w1_codes_122": 13 * KIB,
-    "rounded_z_0_256": 22 * KIB,
-    "left_7_256": 22 * KIB,
-    "left_7_384": 23 * KIB,
-    "tab_words_0": 48 * KIB,
-    "products_1": 48 * KIB,
-    "tab_words_1": 56 * KIB,
-    "y_0": 56 * KIB,
-    "y_1": 58 * KIB,
-    "y_2": 60 * KIB,
-    "y_3": 62 * KIB,
-}
-FIRST_BANKS = [0, 1, 2, 3, 1, 4, 5, 6, 7, 0, 2, 3, 1, 4, 5, 6, 7]
-SECOND_BANKS = [0, 2, 3, 1, 4, 5, 6]
+ALIGN = 64
 
 
 def tile_list_echo_chamber_contrast_kernel(
@@ -76,17 +45,29 @@ def tile_list_echo_chamber_contrast_kernel(
     nc = tc.nc
     with ExitStack() as ctx:
         held = ctx.enter_context(tc.tile_pool(name="held", bufs=1))
-        reused = ctx.enter_context(tc.tile_pool(name="reused", bufs=1))
+        shared = ctx.enter_context(tc.tile_pool(name="shared", bufs=1))
         ring = ctx.enter_context(tc.tile_pool(name="ring", bufs=3))
         psum = ctx.enter_context(tc.psum_pool(name="psum", bufs=1))
 
-        def tile(shape, dtype, name):
-            if name in PLACES:
-                return reused.tile(shape, dtype, name=name, align_bytes=64, offset=PLACES[name])
-            kind = name.split("_")[0]
-            if kind in RING_KINDS:
-                return ring.tile(shape, dtype, name=name, tag=kind, bufs=4, align_bytes=64)
-            return held.tile(shape, dtype, name=name, align_bytes=64)
+        starts = {"free": 0}
+
+        def reserve(name, size):
+            starts[name] = starts["free"]
+            starts["free"] = starts["free"] + size
+
+        def tile(shape, dtype, name, on=None, at=0, lend=False, kind=None):
+            if lend:
+                reserve(name, math.prod(shape[1:]) * BYTES_OF[dtype])
+            if on is not None:
+                starts[name] = starts[on] + at
+            if name in starts:
+                return shared.tile(shape, dtype, name=name, align_bytes=ALIGN, offset=starts[name])
+            if kind is not None:
+                return ring.tile(shape, dtype, name=name, tag=kind, bufs=RING, align_bytes=ALIGN)
+            return held.tile(shape, dtype, name=name, align_bytes=ALIGN)
+
+        def entries(list_sb, j0, j1):
+            return list_sb[:, j0 // LIST_ROWS : j1 // LIST_ROWS]
 
         def load_list(name, src):
             t = held.tile(list(src.shape), U16, name=name)
@@ -94,22 +75,23 @@ def tile_list_echo_chamber_contrast_kernel(
             return t
 
         def load_table_words(a):
-            t = tile([P, T], I32, "tab_words_%d" % a)
+            t = tile([P, T], I32, "tab_words_%d" % a, lend=True)
             nc.sync.dma_start(t[:], tab_words[a].rearrange("p t i -> p (t i)").bitcast(I32))
             return t
 
-        def load_w1(a, g):
-            c0, c1 = COLUMN_GROUPS[g]
-            t = tile([P, PACK, c1 - c0], F32, "raw_%d%d" % (a, g))
-            rows = w1[a * PASS : (a + 1) * PASS, c0:c1]
-            nc.sync.dma_start(t[:], rows.rearrange("(p j) c -> p j c", j=PACK))
-            return t
+        raw = {}
 
-        def load_folded_columns(name, vec):
+        def load_w1(a, g, on=None, at=0):
+            c0, c1 = COLUMN_GROUPS[g]
+            raw[a, g] = tile([P, PACK, c1 - c0], F32, "raw_%d%d" % (a, g), on, at, lend=on is None)
+            rows = w1[a * PASS : (a + 1) * PASS, c0:c1]
+            nc.sync.dma_start(raw[a, g][:], rows.rearrange("(p j) c -> p j c", j=PACK))
+
+        def load_stacked_columns(name, vec):
             t = held.tile([P, 2, 3], F32, name=name)
-            rows = vec[0:PASS].rearrange("(g j t) -> j g t", g=2, t=PACK)
-            nc.scalar.dma_start(t[0:HALF_P, :, :], rows[:, :, 0:3])
-            nc.scalar.dma_start(t[HALF_P:P, :, :], rows[:, :, 1:4])
+            rows = vec[0:PASS].rearrange("(g m t) -> m g t", g=2, t=PACK)
+            for e in range(2):
+                nc.scalar.dma_start(t[e * HALF_P : (e + 1) * HALF_P, :, :], rows[:, :, e : e + 3])
             return t
 
         def load_plain_columns(queue, name, vec):
@@ -119,77 +101,80 @@ def tile_list_echo_chamber_contrast_kernel(
 
         tab_planes = tile([P, T], U8, "tab_planes")
         nc.vector.memset(tab_planes[:].bitcast(I32), 0)
-        gain_folded = load_folded_columns("gain_folded", gain)
+        gain_stacked = load_stacked_columns("gain_stacked", gain)
         gain_plain = load_plain_columns(nc.scalar, "gain_plain", gain)
-        phase_folded = load_folded_columns("phase_folded", phase)
+        phase_stacked = load_stacked_columns("phase_stacked", phase)
         warm = held.tile([P, 2], F32, name="warm")
         nc.vector.memset(warm[:, 0:1], 0.0)
         nc.scalar.activation(warm[:, 1:2], warm[:, 0:1], ACT.Sin)
 
         offs_sb = load_list("offs_sb", offs)
         words = [load_table_words(0), load_table_words(1)]
-        raw = {(0, 0): load_w1(0, 0)}
-        for q in range(4):
+        late_rows = len(SLICES) - EARLY_GAIN_ROWS
+        reserve("late_gain_rows", late_rows * 4 * PAIRS)
+        load_w1(0, 0, "late_gain_rows", KIB)
+        for q in range(P // QUADRANT):
             nc.sync.dma_start(
-                tab_planes[32 * q : 32 * q + 4 * K_PASSES, :].bitcast(I32),
+                tab_planes[QUADRANT * q : QUADRANT * q + 4 * K_PASSES, :].bitcast(I32),
                 tab_scales[:, 4 * q : 4 * q + 4, :].bitcast(I32),
             )
-        raw[1, 0] = load_w1(1, 0)
         words.append(load_table_words(2))
-        raw[2, 0] = load_w1(2, 0)
+        load_w1(1, 0)
+        load_w1(2, 0)
         for a in range(K_PASSES):
-            raw[a, 1] = load_w1(a, 1)
+            load_w1(a, 1)
         pos1_sb = load_list("pos1_sb", pos1)
         pos2_sb = load_list("pos2_sb", pos2)
-        phase_plain = load_plain_columns(nc.sync, "phase_plain", phase)
         for a in range(K_PASSES):
-            raw[a, 2] = load_w1(a, 2)
+            load_w1(a, 2)
+        phase_plain = load_plain_columns(nc.sync, "phase_plain", phase)
         w2_codes = tile([P, H_PASSES, 2 * N], U8, "w2_codes")
         nc.sync.dma_start(w2_codes[:].bitcast(I32), w2_words.rearrange("b p c -> p b c").bitcast(I32))
         pos3_sb = load_list("pos3_sb", pos3)
         pos4_sb = load_list("pos4_sb", pos4)
         w2_planes = tile([P, H_PASSES, N], U8, "w2_planes")
         nc.vector.memset(w2_planes[:].bitcast(I32), 0)
-        for q in range(4):
+        for q in range(P // QUADRANT):
             nc.sync.dma_start(
-                w2_planes[32 * q : 32 * q + 4, :, :].bitcast(I32),
+                w2_planes[QUADRANT * q : QUADRANT * q + 4, :, :].bitcast(I32),
                 w2_scales[:, 4 * q : 4 * q + 4, :].rearrange("b r c -> r b c").bitcast(I32),
             )
 
-        gain_rows = [tile([P, GAIN_WIDTH], F32, "gain_row_%d" % s) for s in range(len(SLICES))]
-        for s in range(len(SLICES)):
+        def column(stacked, plain, s):
             g, u = SLICES[s]
-            column = gain_folded[:, g, 2 * u : 2 * u + 1] if g < 2 else gain_plain[:, u : u + 1]
-            nc.scalar.copy(gain_rows[s][:], column.to_broadcast([P, GAIN_WIDTH]))
+            return stacked[:, g, 2 * u : 2 * u + 1] if g < 2 else plain[:, u : u + 1]
 
-        def phase_column(s):
-            g, u = SLICES[s]
-            return phase_folded[:, g, 2 * u : 2 * u + 1] if g < 2 else phase_plain[:, u : u + 1]
+        gain_rows = {}
+
+        def spread_gain(s):
+            late = s - EARLY_GAIN_ROWS
+            on = "late_gain_rows" if late >= 0 else None
+            gain_rows[s] = tile([P, PAIRS], F32, "gain_row_%d" % s, on, late * 4 * PAIRS)
+            nc.scalar.copy(gain_rows[s][:], column(gain_stacked, gain_plain, s).to_broadcast([P, PAIRS]))
 
         v_codes = {}
         v_planes = tile([P, S], U8, "v_planes")
 
-        def gather_words(a, j0, j1):
-            v_codes[a, j0, j1] = tile([P, j1 - j0], U32, "v_codes_%d_%d" % (a, j0))
-            picks = offs_sb[:, j0 // 16 : j1 // 16]
-            nc.vector.tensor_copy(v_codes[a, j0, j1][:], words[a][:].bitcast(U32).indirect(picks))
+        def gather_words(a):
+            v_codes[a] = tile([P, S], U32, "v_codes_%d" % a)
+            nc.vector.tensor_copy(v_codes[a][:], words[a][:].bitcast(U32).indirect(offs_sb[:]))
 
         rounded, w1_codes, w1_planes = {}, {}, {}
 
-        def round_w1(copy, a, g, t0=0, t1=PACK):
-            c0, c1 = COLUMN_GROUPS[g]
-            rounded[a, g, t0] = tile([P, (t1 - t0) * (c1 - c0)], BF16, "rounded_%d%d%d" % (a, g, t0))
+        def round_w1(copy, a, g, ts, on=None):
+            (c0, c1), (t0, t1) = COLUMN_GROUPS[g], ts
+            rounded[a, g, ts] = tile([P, (t1 - t0) * (c1 - c0)], BF16, "rounded_%d%d%d" % (a, g, t0), on)
             copy(
-                rounded[a, g, t0][:].rearrange("p (u e m j) -> p u m j e", u=(t1 - t0) // 2, e=2, j=PACK),
+                rounded[a, g, ts][:].rearrange("p (u e m j) -> p u m j e", u=(t1 - t0) // 2, e=2, j=PACK),
                 raw[a, g][:].rearrange("p j (m u e) -> p u m j e", u=2, e=2)[:, t0 // 2 : t1 // 2],
             )
 
-        def quantise_w1(a, g, t0=0, t1=PACK):
-            c0, c1 = COLUMN_GROUPS[g]
+        def quantise_w1(a, g, ts, on=None, at=0):
+            (c0, c1), (t0, t1) = COLUMN_GROUPS[g], ts
             width = (t1 - t0) * (c1 - c0) // PACK
-            codes = tile([P, width], U32, "w1_codes_%d%d%d" % (a, g, t0))
+            codes = tile([P, width], U32, "w1_codes_%d%d%d" % (a, g, t0), on, at)
             plane = tile([P, width], U8, "w1_plane_%d%d%d" % (a, g, t0))
-            nc.vector.quantize_mx(codes[:].bitcast(FP8X4), plane[:], rounded[a, g, t0][:])
+            nc.vector.quantize_mx(codes[:].bitcast(FP8X4), plane[:], rounded[a, g, ts][:])
             first = t0 * (c1 - c0) // PASS
             for u in range(width // P):
                 w1_codes[a, g, first + u] = codes[:, u * P : (u + 1) * P]
@@ -198,70 +183,67 @@ def tile_list_echo_chamber_contrast_kernel(
         def bank(number, name):
             return psum.tile([P, BANK], F32, name=name, offset=number * 4 * BANK)
 
-        banks, folded, h_rows, lefts = {}, {}, {}, {}
+        h_rows, lefts = {}, {}
 
-        def first_product(s, j0, j1, passes=range(K_PASSES)):
+        def first_product(s, j0, passes):
             g, u = SLICES[s]
-            if (s, j0) not in banks:
-                banks[s, j0] = bank(FIRST_BANKS[len(banks)], "bank_%d_%d" % (s, j0))
+            sums = bank((2 * s + j0 // BANK) % BANKS, "bank_%d_%d" % (s, j0))
             for a in passes:
-                for (held_a, c0, c1), codes in v_codes.items():
-                    lo, hi = max(j0, c0), min(j1, c1)
-                    if held_a == a and lo < hi:
-                        nc.tensor.matmul_mx(
-                            banks[s, j0][:, lo - j0 : hi - j0],
-                            lhsT=w1_codes[a, g, u].bitcast(FP8X4),
-                            lhsT_scale=w1_planes[a, g, u],
-                            rhs=codes[:, lo - c0 : hi - c0].bitcast(FP8X4),
-                            rhs_scale=v_planes[4 * a : P, lo:hi],
-                            start=(a == 0),
-                            stop=(a == K_PASSES - 1 and hi == j1),
-                        )
+                nc.tensor.matmul_mx(
+                    sums[:],
+                    lhsT=w1_codes[a, g, u].bitcast(FP8X4),
+                    lhsT_scale=w1_planes[a, g, u],
+                    rhs=v_codes[a][:, j0 : j0 + BANK].bitcast(FP8X4),
+                    rhs_scale=v_planes[4 * a : P, j0 : j0 + BANK],
+                    start=(a == passes[0]),
+                    stop=(a == passes[-1]),
+                )
+            return sums
 
-        def fold(s, j0, j1):
-            folded[s, j0] = tile([P, j1 - j0], F32, "folded_%d_%d" % (s, j0))
-            nc.scalar.activation(folded[s, j0][:], banks[s, j0][:, 0 : j1 - j0], ACT.Abs, bias=phase_column(s))
-
-        def sine(s, j0, j1):
-            if s not in h_rows:
-                h_rows[s] = tile([P, S], F32, "h_%d" % s)
-            nc.scalar.activation(h_rows[s][:, j0:j1], folded[s, j0][:], ACT.Sin, bias=math.pi / 2, scale=-1.0)
-
-        def cosine(s):
+        def cosine(s, high_passes=(0, 1, 2), on=None, low_at=0, high_at=0, lend=None):
+            sums = {0: first_product(s, 0, (0, 1, 2)), BANK: first_product(s, BANK, high_passes)}
+            bias = column(phase_stacked, phase_plain, s)
+            sizes = {}
+            for j0, at in ((0, low_at), (BANK, high_at)):
+                sizes[j0] = tile([P, BANK], F32, "size_%d_%d" % (s, j0), on, at, lend == j0, "size")
+                nc.scalar.activation(sizes[j0][:], sums[j0][:], ACT.Abs, bias=bias)
+            h_rows[s] = tile([P, S], F32, "h_%d" % s, kind="h")
             for j0 in (0, BANK):
-                first_product(s, j0, j0 + BANK)
-            for j0 in (0, BANK):
-                fold(s, j0, j0 + BANK)
-            for j0 in (0, BANK):
-                sine(s, j0, j0 + BANK)
+                nc.scalar.activation(h_rows[s][:, j0 : j0 + BANK], sizes[j0][:], ACT.Sin, bias=math.pi / 2, scale=-1.0)
 
         z_codes = [tile([P, PAIRS], U32, "z_codes_%d" % b) for b in range(H_PASSES)]
         z_planes = [tile([P, PAIRS], U8, "z_plane_%d" % b) for b in range(H_PASSES)]
-        products = [tile([P, PACK, PAIRS], F32, "products_%d" % b) for b in range(H_PASSES)]
-        spare = tile([P, 2, PAIRS], F32, "spare")
+        products = [
+            tile([P, PACK, PAIRS], F32, "products_0", lend=True),
+            tile([P, PACK, PAIRS], F32, "products_1", "tab_words_0"),
+        ]
+        spare = tile([P, 2, PAIRS], F32, "spare", "raw_12")
         targets = [products[0][:, 0, :], products[0][:, 1, :], spare[:, 0, :], spare[:, 1, :]]
         targets = targets + [products[1][:, t, :] for t in range(PACK)]
 
-        def first_factor(s, m0=0, m1=PAIRS):
-            lefts[s, m0] = tile([P, m1 - m0], F32, "left_%d_%d" % (s, m0))
-            picks = pos1_sb[:, m0 // 16 : m1 // 16]
-            nc.vector.tensor_tensor(lefts[s, m0][:], h_rows[s][:].indirect(picks), gain_rows[s][:, 0 : m1 - m0], ALU.mult)
+        def first_factor(s, m0=0, m1=PAIRS, on=None, at=0):
+            left = tile([P, m1 - m0], F32, "left_%d_%d" % (s, m0), on, at, kind="left")
+            picked = h_rows[s][:].indirect(entries(pos1_sb, m0, m1))
+            nc.vector.tensor_tensor(left[:], picked, gain_rows[s][:, 0 : m1 - m0], ALU.mult)
+            lefts[s, m0] = left
 
-        def pair_product(s, m0=0, m1=PAIRS):
-            picks = pos2_sb[:, m0 // 16 : m1 // 16]
-            nc.vector.tensor_tensor(targets[s][:, m0:m1], h_rows[s][:].indirect(picks), lefts[s, m0][:], ALU.mult)
+        def pair_product(s, m0=0, m1=PAIRS, left_from=None):
+            left_from = m0 if left_from is None else left_from
+            left = lefts[s, left_from][:, m0 - left_from : m1 - left_from]
+            picked = h_rows[s][:].indirect(entries(pos2_sb, m0, m1))
+            nc.vector.tensor_tensor(targets[s][:, m0:m1], picked, left, ALU.mult)
 
-        def pairs_in_halves(s, m0=0, m1=PAIRS):
+        def pairs_in_halves(s, m0=0, m1=PAIRS, on=None):
             mid = (m0 + m1) // 2
-            first_factor(s, m0, mid)
-            first_factor(s, mid, m1)
+            first_factor(s, m0, mid, on)
+            first_factor(s, mid, m1, on, KIB)
             pair_product(s, m0, mid)
             pair_product(s, mid, m1)
 
         rounded_z = {}
 
-        def round_z(copy, b, m0, m1):
-            rounded_z[b, m0] = tile([P, PACK * (m1 - m0)], BF16, "rounded_z_%d_%d" % (b, m0))
+        def round_z(copy, b, m0, m1, on=None):
+            rounded_z[b, m0] = tile([P, PACK * (m1 - m0)], BF16, "rounded_z_%d_%d" % (b, m0), on)
             order = "p (e u) (c i) -> p c u e i" if b == 0 else "p (u e) (c i) -> p c u e i"
             copy(
                 rounded_z[b, m0][:].rearrange("p (c i u e) -> p c u e i", i=4, u=2, e=2),
@@ -271,104 +253,100 @@ def tile_list_echo_chamber_contrast_kernel(
         def quantise_z(b, m0, m1):
             nc.vector.quantize_mx(z_codes[b][:, m0:m1].bitcast(FP8X4), z_planes[b][:, m0:m1], rounded_z[b, m0][:])
 
-        y_rows = [tile([P, PAIRS], F32, "y_%d" % i) for i in range(N // P)]
-        y_banks = {}
+        y_rows = [tile([P, PAIRS], F32, "y_%d" % i, "tab_words_1", i * 4 * PAIRS) for i in range(N // P)]
+        y_banks = []
 
-        def second_product(i, c0, c1, b, m0, m1, start, stop):
-            if (i, c0) not in y_banks:
-                y_banks[i, c0] = bank(SECOND_BANKS[len(y_banks)], "y_bank_%d_%d" % (i, c0))
-            nc.tensor.matmul_mx(
-                y_banks[i, c0][:, m0 - c0 : m1 - c0],
-                lhsT=w2_codes[:, b, 2 * i * P : 2 * (i + 1) * P].bitcast(FP4X4),
-                lhsT_scale=w2_planes[:, b, i * P : (i + 1) * P],
-                rhs=z_codes[b][:, m0:m1].bitcast(FP8X4),
-                rhs_scale=z_planes[b][:, m0:m1],
-                start=start,
-                stop=stop,
-            )
-
-        def copy_y(i, c0, c1):
-            nc.scalar.copy(y_rows[i][:, c0:c1], y_banks[i, c0][:, 0 : c1 - c0])
-
+        def y_piece(i, c0, c1, widths):
+            y_banks.append(bank(len(y_banks), "y_bank_%d_%d" % (i, c0)))
+            for b in range(H_PASSES):
+                for m0 in range(c0, c1, widths[b]):
+                    m1 = m0 + widths[b]
+                    nc.tensor.matmul_mx(
+                        y_banks[-1][:, m0 - c0 : m1 - c0],
+                        lhsT=w2_codes[:, b, 2 * i * P : 2 * (i + 1) * P].bitcast(FP4X4),
+                        lhsT_scale=w2_planes[:, b, i * P : (i + 1) * P],
+                        rhs=z_codes[b][:, m0:m1].bitcast(FP8X4),
+                        rhs_scale=z_planes[b][:, m0:m1],
+                        start=(b == 0 and m0 == c0),
+                        stop=(b == H_PASSES - 1 and m1 == c1),
+                    )
+            nc.scalar.copy(y_rows[i][:, c0:c1], y_banks[-1][:, 0 : c1 - c0])
 
         on_scalar, on_vector = nc.scalar.copy, nc.vector.tensor_copy
-        gather_words(0, 0, S)
-        gather_words(1, 0, S)
+
+        for s in range(PACK):
+            spread_gain(s)
+        gather_words(0)
+        gather_words(1)
+        round_w1(on_scalar, 0, 0, ALL_T)
+        quantise_w1(0, 0, ALL_T)
         nc.vector.tensor_copy(v_planes[:], tab_planes[:].indirect(offs_sb[:]))
+        for s in range(PACK, len(SLICES)):
+            spread_gain(s)
+        gather_words(2)
+        for a in (1, 2):
+            round_w1(on_scalar, a, 0, LOW_T)
+            round_w1(on_scalar, a, 0, HIGH_T)
+        quantise_w1(1, 0, LOW_T)
+        quantise_w1(2, 0, LOW_T)
+        quantise_w1(1, 0, HIGH_T, "raw_20")
+        quantise_w1(2, 0, HIGH_T)
+        cosine(0, high_passes=(0, 2, 1), lend=BANK)
+
         for a in range(K_PASSES - 1):
-            round_w1(on_scalar, a, 0)
-            quantise_w1(a, 0)
-        gather_words(2, 0, 512)
-        gather_words(2, 512, 768)
-        round_w1(on_scalar, 2, 0, 0, 2)
-        round_w1(on_scalar, 2, 0, 2, 4)
-        quantise_w1(2, 0, 0, 2)
-        gather_words(2, 768, S)
-        quantise_w1(2, 0, 2, 4)
-        for j0, j1 in ((0, 512), (512, 768), (768, S)):
-            first_product(0, j0, j1, range(2))
-        for j0, j1 in ((0, 512), (512, 768), (768, S)):
-            first_product(0, j0, j1, range(2, 3))
-        fold(0, 0, 512)
-        fold(0, 512, 768)
-        sine(0, 0, 512)
-        fold(0, 768, S)
-        sine(0, 512, 768)
-        sine(0, 768, S)
-        for a in range(K_PASSES - 1):
-            round_w1(on_vector, a, 1)
-            quantise_w1(a, 1)
-        round_w1(on_vector, 2, 1)
+            round_w1(on_vector, a, 1, LOW_T)
+            round_w1(on_vector, a, 1, HIGH_T)
+            quantise_w1(a, 1, LOW_T)
+            quantise_w1(a, 1, HIGH_T)
+        round_w1(on_vector, 2, 1, ALL_T)
         cosine(1)
         first_factor(0)
-        quantise_w1(2, 1)
+        quantise_w1(2, 1, ALL_T, "size_0_512")
         pair_product(0)
-        round_w1(on_scalar, 0, 2)
-        pairs_in_halves(1)
+
+        round_w1(on_scalar, 0, 2, LOW_T)
+        round_w1(on_scalar, 0, 2, HIGH_T)
+        pairs_in_halves(1, on="raw_21")
         nc.sync.dma_start(products[0][0:HALF_P, 2:4, :], products[0][HALF_P:P, 0:2, :])
-        round_w1(on_vector, 1, 2, 0, 2)
-        cosine(2)
-        quantise_w1(0, 2)
-        quantise_w1(1, 2, 0, 2)
-        round_w1(on_scalar, 1, 2, 2, 4)
+        quantise_w1(0, 2, LOW_T)
+        round_w1(on_vector, 1, 2, LOW_T)
+        cosine(2, on="raw_02", low_at=6 * KIB, high_at=KIB)
+        quantise_w1(0, 2, HIGH_T, "size_2_0")
+        quantise_w1(1, 2, LOW_T, "size_2_0", KIB)
+        round_w1(on_scalar, 1, 2, HIGH_T)
         first_factor(2)
-        round_w1(on_vector, 2, 2, 0, 2)
-        pair_product(2)
-        quantise_w1(2, 2, 0, 2)
-        cosine(3)
-        round_w1(on_scalar, 2, 2, 2, 4)
+        round_w1(on_vector, 2, 2, LOW_T)
+        pair_product(2, 0, HALF)
+        quantise_w1(2, 2, LOW_T)
+        pair_product(2, HALF, PAIRS, left_from=0)
+        cosine(3, on="raw_02", low_at=0, high_at=2 * KIB)
+        round_w1(on_scalar, 2, 2, HIGH_T, "size_3_0")
         first_factor(3)
-        quantise_w1(1, 2, 2, 4)
+        quantise_w1(1, 2, HIGH_T, "size_3_512")
         pair_product(3)
         nc.sync.dma_start(products[0][HALF_P:P, 0:2, :], spare[0:HALF_P, :, :])
         nc.sync.dma_start(products[0][HALF_P:P, 2:4, :], spare[HALF_P:P, :, :])
-        quantise_w1(2, 2, 2, 4)
-        for s in (4, 5, 6):
-            cosine(s)
-            pairs_in_halves(s)
-        round_z(on_scalar, 0, 0, HALF)
-        quantise_z(0, 0, HALF)
-        cosine(7)
+        quantise_w1(2, 2, HIGH_T)
 
         last = len(SLICES) - 1
-        q3 = HALF + QUARTER
+        for s in range(PACK, last):
+            cosine(s, lend=0 if s == last - 1 else None)
+            pairs_in_halves(s)
+        round_z(on_scalar, 0, 0, HALF, "size_%d_0" % (last - 1))
+        quantise_z(0, 0, HALF)
+        cosine(last)
         round_z(on_scalar, 0, HALF, PAIRS)
         pairs_in_halves(last, 0, HALF)
         quantise_z(0, HALF, PAIRS)
+
+        q3 = HALF + QUARTER
         round_z(on_scalar, 1, 0, HALF)
-        pairs_in_halves(last, HALF, PAIRS)
+        pairs_in_halves(last, HALF, PAIRS, "products_0")
         round_z(on_scalar, 1, HALF, q3)
         quantise_z(1, 0, HALF)
         round_z(on_vector, 1, q3, PAIRS)
         quantise_z(1, HALF, q3)
         quantise_z(1, q3, PAIRS)
-
-        def y_piece(i, c0, c1, widths):
-            for b in range(H_PASSES):
-                for m0 in range(c0, c1, widths[b]):
-                    m1 = m0 + widths[b]
-                    second_product(i, c0, c1, b, m0, m1, b == 0 and m0 == c0, b == H_PASSES - 1 and m1 == c1)
-            copy_y(i, c0, c1)
 
         y_piece(0, 0, HALF, (HALF, HALF))
         y_piece(0, HALF, q3, (QUARTER, QUARTER))
@@ -377,15 +355,16 @@ def tile_list_echo_chamber_contrast_kernel(
         y_piece(1, HALF, PAIRS, (HALF, HALF))
         for i in range(2, N // P):
             y_piece(i, 0, PAIRS, (HALF, PAIRS))
+
         for i in range(N // P):
             one_side = ring.tile([P, CONTRASTS], F32, name="one_side")
             nc.vector.tensor_copy(one_side[:], y_rows[i][:].indirect(pos3_sb[:]))
             width = CONTRASTS // 2 if i == N // P - 1 else CONTRASTS
             for j0 in range(0, CONTRASTS, width):
                 diff = ring.tile([P, width], F32, name="diff" if j0 == 0 else "diff_last", bufs=2)
-                picks = pos4_sb[:, j0 // 16 : (j0 + width) // 16]
-                nc.vector.tensor_tensor(diff[:], y_rows[i][:].indirect(picks), one_side[:, j0 : j0 + width], ALU.subtract)
-                squared = ring.tile([P, width], F32, name="squared", bufs=5)
+                picked = y_rows[i][:].indirect(entries(pos4_sb, j0, j0 + width))
+                nc.vector.tensor_tensor(diff[:], picked, one_side[:, j0 : j0 + width], ALU.subtract)
+                squared = ring.tile([P, width], F32, name="squared", bufs=N // P + 1)
                 nc.scalar.activation(squared[:], diff[:], ACT.Square)
                 queue = nc.scalar if (i, j0 + width) == (N // P - 1, CONTRASTS) else nc.sync
                 queue.dma_start(out[i * P : (i + 1) * P, j0 : j0 + width], squared[:])

@@ -280,7 +280,8 @@ def tile_list_echo_chamber_contrast_kernel(
         gather_words(1)
         round_w1(on_scalar, 0, 0, ALL_T)
         quantise_w1(0, 0, ALL_T)
-        nc.vector.tensor_copy(v_planes[:], tab_planes[:].indirect(offs_sb[:]))
+        for j0 in (0, BANK):
+            nc.vector.tensor_copy(v_planes[:, j0 : j0 + BANK], tab_planes[:].indirect(entries(offs_sb, j0, j0 + BANK)))
         for s in range(PACK, len(SLICES)):
             spread_gain(s)
         gather_words(2)

@@ -36,7 +36,7 @@ LOW_T, HIGH_T, ALL_T = (0, 2), (2, 4), (0, 4)
 EARLY_GAIN_ROWS = 5
 RING = 4
 KIB = 1024
-ALIGN = 64
+ALIGN = 256
 
 
 def tile_list_echo_chamber_contrast_kernel(
@@ -358,14 +358,14 @@ def tile_list_echo_chamber_contrast_kernel(
             y_piece(i, 0, PAIRS, (HALF, PAIRS))
 
         for i in range(N // P):
-            one_side = ring.tile([P, CONTRASTS], F32, name="one_side")
+            one_side = ring.tile([P, CONTRASTS], F32, name="one_side", align_bytes=ALIGN)
             nc.vector.tensor_copy(one_side[:], y_rows[i][:].indirect(pos3_sb[:]))
             width = CONTRASTS // 2 if i == N // P - 1 else CONTRASTS
             for j0 in range(0, CONTRASTS, width):
-                diff = ring.tile([P, width], F32, name="diff" if j0 == 0 else "diff_last", bufs=2)
+                diff = ring.tile([P, width], F32, name="diff" if j0 == 0 else "diff_last", bufs=2, align_bytes=ALIGN)
                 picked = y_rows[i][:].indirect(entries(pos4_sb, j0, j0 + width))
                 nc.vector.tensor_tensor(diff[:], picked, one_side[:, j0 : j0 + width], ALU.subtract)
-                squared = ring.tile([P, width], F32, name="squared", bufs=N // P + 1)
+                squared = ring.tile([P, width], F32, name="squared", bufs=N // P + 1, align_bytes=ALIGN)
                 nc.scalar.activation(squared[:], diff[:], ACT.Square)
                 queue = nc.scalar if (i, j0 + width) == (N // P - 1, CONTRASTS) else nc.sync
                 queue.dma_start(out[i * P : (i + 1) * P, j0 : j0 + width], squared[:])

import math
from contextlib import ExitStack

import concourse.mybir as mybir

K, H, N, T, S, PAIRS, CONTRASTS = 1536, 1024, 512, 2048, 1024, 512, 256
FLOPS = 2 * K * H * S + 2 * H * N * PAIRS

F32 = mybir.dt.float32
BF16 = mybir.dt.bfloat16
I32 = mybir.dt.int32
U32 = mybir.dt.uint32
U16 = mybir.dt.uint16
U8 = mybir.dt.uint8
FP8X4 = mybir.dt.float8_e4m3fn_x4
FP4X4 = mybir.dt.float4_e2m1fn_x4
ACT = mybir.ActivationFunctionType
ALU = mybir.AluOpType
BYTES_OF = {F32: 4, I32: 4, U32: 4, BF16: 2, U8: 1}

P = 128
HALF_P = P // 2
QUADRANT = 32
PACK = 4
PASS = P * PACK
BANK = 512
BANKS = 8
LIST_ROWS = 16
K_PASSES = K // PASS
H_PASSES = H // PASS
HALF = PAIRS // 2
QUARTER = PAIRS // 4
COLUMN_GROUPS = [(0, 256), (256, 512), (512, 1024)]
SLICES = [(g, u) for g in range(2) for u in range(2)] + [(2, t) for t in range(PACK)]
LOW_T, HIGH_T, ALL_T = (0, 2), (2, 4), (0, 4)
EARLY_GAIN_ROWS = 5
RING = 4
KIB = 1024
ALIGN = 256


def tile_list_echo_chamber_contrast_kernel(
    tc, tab_words, tab_scales, offs, w1, phase, gain, pos1, pos2, w2_words, w2_scales, pos3, pos4, out
):
    nc = tc.nc
    with ExitStack() as ctx:
        held = ctx.enter_context(tc.tile_pool(name="held", bufs=1))
        shared = ctx.enter_context(tc.tile_pool(name="shared", bufs=1))
        ring = ctx.enter_context(tc.tile_pool(name="ring", bufs=3))
        psum = ctx.enter_context(tc.psum_pool(name="psum", bufs=1))

        starts = {"free": 0}

        def reserve(name, size):
            starts[name] = starts["free"]
            starts["free"] = starts["free"] + size

        def tile(shape, dtype, name, on=None, at=0, lend=False, kind=None):
            if lend:
                reserve(name, math.prod(shape[1:]) * BYTES_OF[dtype])
            if on is not None:
                starts[name] = starts[on] + at
            if name in starts:
                return shared.tile(shape, dtype, name=name, align_bytes=ALIGN, offset=starts[name])
            if kind is not None:
                return ring.tile(shape, dtype, name=name, tag=kind, bufs=RING, align_bytes=ALIGN)
            return held.tile(shape, dtype, name=name, align_bytes=ALIGN)

        def entries(list_sb, j0, j1):
            return list_sb[:, j0 // LIST_ROWS : j1 // LIST_ROWS]

        def load_list(name, src):
            t = held.tile(list(src.shape), U16, name=name)
            nc.sync.dma_start(t[:], src)
            return t

        def load_table_words(a):
            t = tile([P, T], I32, "tab_words_%d" % a, lend=True)
            nc.sync.dma_start(t[:], tab_words[a].rearrange("p t i -> p (t i)").bitcast(I32))
            return t

        raw = {}

        def load_w1(a, g, on=None, at=0):
            c0, c1 = COLUMN_GROUPS[g]
            raw[a, g] = tile([P, PACK, c1 - c0], F32, "raw_%d%d" % (a, g), on, at, lend=on is None)
            rows = w1[a * PASS : (a + 1) * PASS, c0:c1]
            nc.sync.dma_start(raw[a, g][:], rows.rearrange("(p j) c -> p j c", j=PACK))

        def load_stacked_columns(name, vec):
            t = held.tile([P, 2, 3], F32, name=name)
            rows = vec[0:PASS].rearrange("(g m t) -> m g t", g=2, t=PACK)
            for e in range(2):
                nc.scalar.dma_start(t[e * HALF_P : (e + 1) * HALF_P, :, :], rows[:, :, e : e + 3])
            return t

        def load_plain_columns(queue, name, vec):
            t = held.tile([P, PACK], F32, name=name)
            queue.dma_start(t[:], vec[PASS : 2 * PASS].rearrange("(p t) -> p t", t=PACK))
            return t

        tab_planes = tile([P, T], U8, "tab_planes")
        nc.vector.memset(tab_planes[:].bitcast(I32), 0)
        gain_stacked = load_stacked_columns("gain_stacked", gain)
        gain_plain = load_plain_columns(nc.scalar, "gain_plain", gain)
        phase_stacked = load_stacked_columns("phase_stacked", phase)
        warm = held.tile([P, 2], F32, name="warm")
        nc.vector.memset(warm[:, 0:1], 0.0)
        nc.scalar.activation(warm[:, 1:2], warm[:, 0:1], ACT.Sin)

        offs_sb = load_list("offs_sb", offs)
        words = [load_table_words(0), load_table_words(1)]
        late_rows = len(SLICES) - EARLY_GAIN_ROWS
        reserve("late_gain_rows", late_rows * 4 * PAIRS)
        load_w1(0, 0, "late_gain_rows", KIB)
        for q in range(P // QUADRANT):
            nc.sync.dma_start(
                tab_planes[QUADRANT * q : QUADRANT * q + 4 * K_PASSES, :].bitcast(I32),
                tab_scales[:, 4 * q : 4 * q + 4, :].bitcast(I32),
            )
        words.append(load_table_words(2))
        load_w1(1, 0)
        load_w1(2, 0)
        for a in range(K_PASSES):
            load_w1(a, 1)
        pos1_sb = load_list("pos1_sb", pos1)
        pos2_sb = load_list("pos2_sb", pos2)
        for a in range(K_PASSES):
            load_w1(a, 2)
        phase_plain = load_plain_columns(nc.sync, "phase_plain", phase)
        w2_codes = tile([P, H_PASSES, 2 * N], U8, "w2_codes")
        nc.sync.dma_start(w2_codes[:].bitcast(I32), w2_words.rearrange("b p c -> p b c").bitcast(I32))
        pos3_sb = load_list("pos3_sb", pos3)
        pos4_sb = load_list("pos4_sb", pos4)
        w2_planes = tile([P, H_PASSES, N], U8, "w2_planes")
        nc.vector.memset(w2_planes[:].bitcast(I32), 0)
        for q in range(P // QUADRANT):
            nc.sync.dma_start(
                w2_planes[QUADRANT * q : QUADRANT * q + 4, :, :].bitcast(I32),
                w2_scales[:, 4 * q : 4 * q + 4, :].rearrange("b r c -> r b c").bitcast(I32),
            )

        def column(stacked, plain, s):
            g, u = SLICES[s]
            return stacked[:, g, 2 * u : 2 * u + 1] if g < 2 else plain[:, u : u + 1]

        gain_rows = {}

        def spread_gain(s):
            late = s - EARLY_GAIN_ROWS
            on = "late_gain_rows" if late >= 0 else None
            gain_rows[s] = tile([P, PAIRS], F32, "gain_row_%d" % s, on, late * 4 * PAIRS)
            nc.scalar.copy(gain_rows[s][:], column(gain_stacked, gain_plain, s).to_broadcast([P, PAIRS]))

        v_codes = {}
        v_planes = tile([P, S], U8, "v_planes")

        def gather_words(a):
            v_codes[a] = tile([P, S], U32, "v_codes_%d" % a)
            nc.vector.tensor_copy(v_codes[a][:], words[a][:].bitcast(U32).indirect(offs_sb[:]))

        rounded, w1_codes, w1_planes = {}, {}, {}

        def round_w1(copy, a, g, ts, on=None):
            (c0, c1), (t0, t1) = COLUMN_GROUPS[g], ts
            rounded[a, g, ts] = tile([P, (t1 - t0) * (c1 - c0)], BF16, "rounded_%d%d%d" % (a, g, t0), on)
            copy(
                rounded[a, g, ts][:].rearrange("p (u e m j) -> p u m j e", u=(t1 - t0) // 2, e=2, j=PACK),
                raw[a, g][:].rearrange("p j (m u e) -> p u m j e", u=2, e=2)[:, t0 // 2 : t1 // 2],
            )

        def quantise_w1(a, g, ts, on=None, at=0):
            (c0, c1), (t0, t1) = COLUMN_GROUPS[g], ts
            width = (t1 - t0) * (c1 - c0) // PACK
            codes = tile([P, width], U32, "w1_codes_%d%d%d" % (a, g, t0), on, at)
            plane = tile([P, width], U8, "w1_plane_%d%d%d" % (a, g, t0))
            nc.vector.quantize_mx(codes[:].bitcast(FP8X4), plane[:], rounded[a, g, ts][:])
            first = t0 * (c1 - c0) // PASS
            for u in range(width // P):
                w1_codes[a, g, first + u] = codes[:, u * P : (u + 1) * P]
                w1_planes[a, g, first + u] = plane[:, u * P : (u + 1) * P]

        def bank(number, name):
            return psum.tile([P, BANK], F32, name=name, offset=number * 4 * BANK)

        h_rows, lefts = {}, {}

        def first_product(s, j0, passes):
            g, u = SLICES[s]
            sums = bank((2 * s + j0 // BANK) % BANKS, "bank_%d_%d" % (s, j0))
            for a in passes:
                nc.tensor.matmul_mx(
                    sums[:],
                    lhsT=w1_codes[a, g, u].bitcast(FP8X4),
                    lhsT_scale=w1_planes[a, g, u],
                    rhs=v_codes[a][:, j0 : j0 + BANK].bitcast(FP8X4),
                    rhs_scale=v_planes[4 * a : P, j0 : j0 + BANK],
                    start=(a == passes[0]),
                    stop=(a == passes[-1]),
                )
            return sums

        def cosine(s, high_passes=(0, 1, 2), on=None, low_at=0, high_at=0, lend=None):
            sums = {0: first_product(s, 0, (0, 1, 2)), BANK: first_product(s, BANK, high_passes)}
            bias = column(phase_stacked, phase_plain, s)
            sizes = {}
            for j0, at in ((0, low_at), (BANK, high_at)):
                sizes[j0] = tile([P, BANK], F32, "size_%d_%d" % (s, j0), on, at, lend == j0, "size")
                nc.scalar.activation(sizes[j0][:], sums[j0][:], ACT.Abs, bias=bias)
            h_rows[s] = tile([P, S], F32, "h_%d" % s, kind="h")
            for j0 in (0, BANK):
                nc.scalar.activation(h_rows[s][:, j0 : j0 + BANK], sizes[j0][:], ACT.Sin, bias=math.pi / 2, scale=-1.0)

        z_codes = [tile([P, PAIRS], U32, "z_codes_%d" % b) for b in range(H_PASSES)]
        z_planes = [tile([P, PAIRS], U8, "z_plane_%d" % b) for b in range(H_PASSES)]
        products = [
            tile([P, PACK, PAIRS], F32, "products_0", lend=True),
            tile([P, PACK, PAIRS], F32, "products_1", "tab_words_0"),
        ]
        spare = tile([P, 2, PAIRS], F32, "spare", "raw_12")
        targets = [products[0][:, 0, :], products[0][:, 1, :], spare[:, 0, :], spare[:, 1, :]]
        targets = targets + [products[1][:, t, :] for t in range(PACK)]

        def first_factor(s, m0=0, m1=PAIRS, on=None, at=0):
            left = tile([P, m1 - m0], F32, "left_%d_%d" % (s, m0), on, at, kind="left")
            picked = h_rows[s][:].indirect(entries(pos1_sb, m0, m1))
            nc.vector.tensor_tensor(left[:], picked, gain_rows[s][:, 0 : m1 - m0], ALU.mult)
            lefts[s, m0] = left

        def pair_product(s, m0=0, m1=PAIRS, left_from=None):
            left_from = m0 if left_from is None else left_from
            left = lefts[s, left_from][:, m0 - left_from : m1 - left_from]
            picked = h_rows[s][:].indirect(entries(pos2_sb, m0, m1))
            nc.vector.tensor_tensor(targets[s][:, m0:m1], picked, left, ALU.mult)

        def pairs_in_halves(s, m0=0, m1=PAIRS, on=None):
            mid = (m0 + m1) // 2
            first_factor(s, m0, mid, on)
            first_factor(s, mid, m1, on, KIB)
            pair_product(s, m0, mid)
            pair_product(s, mid, m1)

        rounded_z = {}

        def round_z(copy, b, m0, m1, on=None):
            rounded_z[b, m0] = tile([P, PACK * (m1 - m0)], BF16, "rounded_z_%d_%d" % (b, m0), on)
            order = "p (e u) (c i) -> p c u e i" if b == 0 else "p (u e) (c i) -> p c u e i"
            copy(
                rounded_z[b, m0][:].rearrange("p (c i u e) -> p c u e i", i=4, u=2, e=2),
                products[b][:, :, m0:m1].rearrange(order, i=4, u=2),
            )

        def quantise_z(b, m0, m1):
            nc.vector.quantize_mx(z_codes[b][:, m0:m1].bitcast(FP8X4), z_planes[b][:, m0:m1], rounded_z[b, m0][:])

        y_rows = [tile([P, PAIRS], F32, "y_%d" % i, "tab_words_1", i * 4 * PAIRS) for i in range(N // P)]
        y_banks = []

        def y_piece(i, c0, c1, widths):
            y_banks.append(bank(len(y_banks), "y_bank_%d_%d" % (i, c0)))
            for b in range(H_PASSES):
                for m0 in range(c0, c1, widths[b]):
                    m1 = m0 + widths[b]
                    nc.tensor.matmul_mx(
                        y_banks[-1][:, m0 - c0 : m1 - c0],
                        lhsT=w2_codes[:, b, 2 * i * P : 2 * (i + 1) * P].bitcast(FP4X4),
                        lhsT_scale=w2_planes[:, b, i * P : (i + 1) * P],
                        rhs=z_codes[b][:, m0:m1].bitcast(FP8X4),
                        rhs_scale=z_planes[b][:, m0:m1],
                        start=(b == 0 and m0 == c0),
                        stop=(b == H_PASSES - 1 and m1 == c1),
                    )
            nc.scalar.copy(y_rows[i][:, c0:c1], y_banks[-1][:, 0 : c1 - c0])

        on_scalar, on_vector = nc.scalar.copy, nc.vector.tensor_copy

        for s in range(PACK):
            spread_gain(s)
        gather_words(0)
        gather_words(1)
        round_w1(on_scalar, 0, 0, ALL_T)
        quantise_w1(0, 0, ALL_T)
        for j0 in (0, BANK):
            nc.vector.tensor_copy(v_planes[:, j0 : j0 + BANK], tab_planes[:].indirect(entries(offs_sb, j0, j0 + BANK)))
        for s in range(PACK, len(SLICES)):
            spread_gain(s)
        gather_words(2)
        for a in (1, 2):
            round_w1(on_scalar, a, 0, LOW_T)
            round_w1(on_scalar, a, 0, HIGH_T)
        quantise_w1(1, 0, LOW_T)
        quantise_w1(2, 0, LOW_T)
        quantise_w1(1, 0, HIGH_T, "raw_20")
        quantise_w1(2, 0, HIGH_T)
        cosine(0, high_passes=(0, 2, 1), lend=BANK)

        for a in range(K_PASSES - 1):
            round_w1(on_vector, a, 1, LOW_T)
            round_w1(on_vector, a, 1, HIGH_T)
            quantise_w1(a, 1, LOW_T)
            quantise_w1(a, 1, HIGH_T)
        round_w1(on_vector, 2, 1, ALL_T)
        cosine(1)
        first_factor(0)
        quantise_w1(2, 1, ALL_T, "size_0_512")
        pair_product(0)

        round_w1(on_scalar, 0, 2, LOW_T)
        round_w1(on_scalar, 0, 2, HIGH_T)
        pairs_in_halves(1, on="raw_21")
        nc.sync.dma_start(products[0][0:HALF_P, 2:4, :], products[0][HALF_P:P, 0:2, :])
        quantise_w1(0, 2, LOW_T)
        round_w1(on_vector, 1, 2, LOW_T)
        cosine(2, on="raw_02", low_at=6 * KIB, high_at=KIB)
        quantise_w1(0, 2, HIGH_T, "size_2_0")
        quantise_w1(1, 2, LOW_T, "size_2_0", KIB)
        round_w1(on_scalar, 1, 2, HIGH_T)
        first_factor(2)
        round_w1(on_vector, 2, 2, LOW_T)
        pair_product(2, 0, HALF)
        quantise_w1(2, 2, LOW_T)
        pair_product(2, HALF, PAIRS, left_from=0)
        cosine(3, on="raw_02", low_at=0, high_at=2 * KIB)
        round_w1(on_scalar, 2, 2, HIGH_T, "size_3_0")
        first_factor(3)
        quantise_w1(1, 2, HIGH_T, "size_3_512")
        pair_product(3)
        nc.sync.dma_start(products[0][HALF_P:P, 0:2, :], spare[0:HALF_P, :, :])
        nc.sync.dma_start(products[0][HALF_P:P, 2:4, :], spare[HALF_P:P, :, :])
        quantise_w1(2, 2, HIGH_T)

        last = len(SLICES) - 1
        for s in range(PACK, last):
            cosine(s, lend=0 if s == last - 1 else None)
            pairs_in_halves(s)
        round_z(on_scalar, 0, 0, HALF, "size_%d_0" % (last - 1))
        quantise_z(0, 0, HALF)
        cosine(last)
        round_z(on_scalar, 0, HALF, PAIRS)
        pairs_in_halves(last, 0, HALF)
        quantise_z(0, HALF, PAIRS)

        q3 = HALF + QUARTER
        round_z(on_scalar, 1, 0, HALF)
        pairs_in_halves(last, HALF, PAIRS, "products_0")
        round_z(on_scalar, 1, HALF, q3)
        quantise_z(1, 0, HALF)
        round_z(on_vector, 1, q3, PAIRS)
        quantise_z(1, HALF, q3)
        quantise_z(1, q3, PAIRS)

        y_piece(0, 0, HALF, (HALF, HALF))
        y_piece(0, HALF, q3, (QUARTER, QUARTER))
        y_piece(0, q3, PAIRS, (QUARTER, QUARTER))
        y_piece(1, 0, HALF, (HALF, HALF))
        y_piece(1, HALF, PAIRS, (HALF, HALF))
        for i in range(2, N // P):
            y_piece(i, 0, PAIRS, (HALF, PAIRS))

        for i in range(N // P):
            one_side = ring.tile([P, CONTRASTS], F32, name="one_side", align_bytes=ALIGN)
            nc.vector.tensor_copy(one_side[:], y_rows[i][:].indirect(pos3_sb[:]))
            width = CONTRASTS // 2 if i == N // P - 1 else CONTRASTS
            for j0 in range(0, CONTRASTS, width):
                diff = ring.tile([P, width], F32, name="diff" if j0 == 0 else "diff_last", bufs=2, align_bytes=ALIGN)
                picked = y_rows[i][:].indirect(entries(pos4_sb, j0, j0 + width))
                nc.vector.tensor_tensor(diff[:], picked, one_side[:, j0 : j0 + width], ALU.subtract)
                squared = ring.tile([P, width], F32, name="squared", bufs=N // P + 1, align_bytes=ALIGN)
                nc.scalar.activation(squared[:], diff[:], ACT.Square)
                queue = nc.scalar if (i, j0 + width) == (N // P - 1, CONTRASTS) else nc.sync
                queue.dma_start(out[i * P : (i + 1) * P, j0 : j0 + width], squared[:])
